import numpy as np
import ml_dtypes


def mxq(x, axis, fmt="e4m3"):
    dtype, down = {"e4m3": (ml_dtypes.float8_e4m3fn, 7), "e5m2": (ml_dtypes.float8_e5m2, 14)}[fmt]
    v = np.moveaxis(np.asarray(x, np.float32).astype(ml_dtypes.bfloat16).astype(np.float64), axis, -1)
    blocks = v.reshape(v.shape[:-1] + (-1, 32))
    amax = np.abs(blocks).max(-1, keepdims=True)
    byte = np.maximum(np.where(amax > 0, np.frexp(amax)[1] - 1 + 127, 0) - down, 1)
    scale = np.exp2(byte - 127.0)
    codes = (blocks / scale).astype(np.float32).astype(dtype).astype(np.float64)
    return np.moveaxis((codes * scale).reshape(v.shape), -1, axis)


WIDE = False


def mx_kscale(k):
    if not WIDE:
        return np.ones(k)
    levels = np.array([10, -10, 5, -5, 0])
    if k % 512:
        return np.exp2(np.random.permutation(np.resize(levels, k // 32))).repeat(32)
    a = np.empty((k // 512, 16))
    for p in range(k // 512):
        a[p, :8] = np.random.permutation(np.resize(levels, 8))
        for g in range(8):
            far = levels[np.abs(levels - a[p, g]) >= 10]
            a[p, g + 8] = far[np.random.randint(len(far))]
    return np.exp2(a.ravel()).repeat(32)


def f64(x):
    return np.asarray(x).astype(np.float64)


def striped(idx):
    return np.tile(idx.reshape(-1, 16).T, (8, 1)).astype(np.uint16)


def unstriped(offs):
    return offs[:16].T.reshape(-1).astype(np.int64)


E2M1 = np.array([0.0, 0.5, 1.0, 1.5, 2.0, 3.0, 4.0, 6.0, -0.0, -0.5, -1.0, -1.5, -2.0, -3.0, -4.0, -6.0])


def pack_weight(w, fmt):
    k, n = w.shape
    w = f64(np.asarray(w, np.float32).astype(ml_dtypes.bfloat16)).reshape(k // 32, 32, n)
    amax = np.abs(w).max(1)
    if fmt == "e4m3":
        byte = np.frexp(amax)[1] - 1 + 127 - 7
    else:
        mant, ex = np.frexp(amax / 6.0)
        byte = np.where(mant > 0.5, ex, ex - 1) + 127
    byte = np.clip(np.where(amax > 0, byte, 1), 1, 254)
    scaled = (w * np.exp2(127.0 - byte)[:, None, :]).reshape(k, n).astype(np.float32)
    by_word = np.ascontiguousarray(scaled.reshape(k // 512, 128, 4, n).transpose(0, 1, 3, 2))
    if fmt == "e4m3":
        words = by_word.astype(ml_dtypes.float8_e4m3fn).view(np.uint8)
    else:
        c = by_word.astype(ml_dtypes.float4_e2m1fn).view(np.uint8) & 0xF
        words = (c[..., 0::2] | (c[..., 1::2] << 4)).reshape(k // 512, 128, 2 * n)
    return np.ascontiguousarray(words), np.ascontiguousarray(byte.astype(np.uint8).reshape(k // 512, 16, n))


def unpack_weight(words, scales, fmt):
    g, _, n = scales.shape
    words = np.ascontiguousarray(words).reshape(g, 128, n, -1)
    if fmt == "e4m3":
        vals = words.view(ml_dtypes.float8_e4m3fn).astype(np.float64)
    else:
        nib = np.empty((g, 128, n, 4), np.uint8)
        nib[..., 0::2] = words & 0xF
        nib[..., 1::2] = words >> 4
        vals = E2M1[nib]
    vals = vals * np.repeat(np.exp2(scales.astype(np.float64) - 127.0), 8, axis=1)[..., None]
    return vals.transpose(0, 1, 3, 2).reshape(g * 512, n)


def gelu(v):
    return 0.5 * v * (1.0 + np.tanh(np.sqrt(2.0 / np.pi) * (v + 0.044715 * v**3)))


K, K2, H, N, T, S, P, T2 = 1024, 512, 512, 512, 2048, 1024, 512, 2048

def setup_inputs():
    n = np.random.standard_normal
    s, s2, u = mx_kscale(K)[:, None], mx_kscale(K2)[:, None], mx_kscale(H)[:, None]
    tab_words, tab_scales = pack_weight((n((K, T)) + 0.5) * s, "e4m3")
    tab2_words, tab2_scales = pack_weight(n((K2, T)) * s2, "e4m3")
    w4_words, w4_scales = pack_weight(0.34 * n((K, H)) / np.sqrt(K) / s, "e2m1")
    w8_words, w8_scales = pack_weight(4.0 * n((H, N)) / np.sqrt(H) / u, "e4m3")
    perm = np.random.permutation(T2)
    return {
        "tab_words": tab_words, "tab_scales": tab_scales,
        "tab2_words": tab2_words, "tab2_scales": tab2_scales,
        "offs": striped(np.random.permutation(T)[:S]),
        "offs2": striped(np.random.permutation(T)[:P]),
        "pos1": striped(np.random.permutation(S)[:P]),
        "offs3": striped(perm[:S]), "offs4": striped(perm[S:S + P]),
        "w4_words": w4_words, "w4_scales": w4_scales,
        "wb": ((0.18 * n((K, H)) / np.sqrt(K) + 2.0 / K) / s).astype(np.float32),
        "wc": (0.28 * n((K2, H)) / np.sqrt(K2) / s2).astype(np.float32),
        "gain": (u[:, 0] * np.exp(0.3 * n(H))).astype(np.float32),
        "wo1": (3.0 * n((H, N)) / np.sqrt(H) / u).astype(np.float32),
        "w8_words": w8_words, "w8_scales": w8_scales,
        "wg1": np.exp(0.3 * n((128, S))).astype(np.float32),
        "wg2": np.exp(0.3 * n((128, P))).astype(np.float32),
        "page1": (0.8 * n((N, T2))).astype(np.float32)}

def reference(tab_words, tab_scales, tab2_words, tab2_scales, offs, offs2, pos1, offs3, offs4,
              w4_words, w4_scales, wb, wc, gain, wo1, w8_words, w8_scales, wg1, wg2, page1):
    v = unpack_weight(tab_words, tab_scales, "e4m3")[:, unstriped(offs)]
    v2 = unpack_weight(tab2_words, tab2_scales, "e4m3")[:, unstriped(offs2)]
    w4 = unpack_weight(w4_words, w4_scales, "e2m1")
    w8 = unpack_weight(w8_words, w8_scales, "e4m3")
    h1 = (w4.T @ v) * (mxq(f64(wb), 0, "e4m3").T @ v)
    h2 = mxq(f64(wc), 0, "e4m3").T @ v2
    z = np.concatenate([np.tanh(h1), np.sin(h2 + h1[:, unstriped(pos1)])], axis=1) * f64(gain)[:, None]
    zq = mxq(z, 0, "e4m3")
    y1 = mxq(f64(wo1), 0, "e4m3").T @ zq[:, :S]
    y2 = w8.T @ zq[:, S:]
    out = f64(page1).copy()
    out[:, unstriped(offs3)] = np.tile(f64(wg1), (N // 128, 1)) * y1
    out[:, unstriped(offs4)] = np.tile(f64(wg2), (N // 128, 1)) * y2
    return out

@@ -1,0 +1,291 @@
+import math
+from contextlib import ExitStack
+
+import concourse.mybir as mybir
+
+F32 = mybir.dt.float32
+BF16 = mybir.dt.bfloat16
+I32 = mybir.dt.int32
+U32 = mybir.dt.uint32
+U16 = mybir.dt.uint16
+U8 = mybir.dt.uint8
+FP8X4 = mybir.dt.float8_e4m3fn_x4
+FP4X4 = mybir.dt.float4_e2m1fn_x4
+ACT = mybir.ActivationFunctionType
+ALU = mybir.AluOpType
+
+K, K2, H, N, T, S, C, T2 = 1024, 512, 512, 512, 2048, 1024, 512, 2048
+P = 128
+PACK = 4
+FLOPS = 2 * (2 * K * H * S + K2 * H * C + H * N * (S + C))
+
+LAYER_BLOCKS = ((0, 256), (256, 512), (512, 1024))
+
+
+def tile_list_treaty_layer_pages_kernel(
+    tc, tab_words, tab_scales, tab2_words, tab2_scales, offs, offs2, pos1, offs3, offs4,
+    w4_words, w4_scales, wb, wc, gain, wo1, w8_words, w8_scales, wg1, wg2, page1, out,
+):
+    nc = tc.nc
+    with ExitStack() as ctx:
+        keep = ctx.enter_context(tc.tile_pool(name="keep", bufs=1))
+        ring = ctx.enter_context(tc.tile_pool(name="ring", bufs=2))
+        psum = ctx.enter_context(tc.psum_pool(name="psum", bufs=2))
+
+        def load_list(src, name):
+            tile = keep.tile(list(src.shape), U16, name=name)
+            nc.sync.dma_start(tile[:], src)
+            return tile
+
+        def zeroed_plane(width, name):
+            tile = keep.tile([P, width], U8, name=name, align_bytes=64)
+            nc.vector.memset(tile[:].bitcast(I32), 0)
+            return tile
+
+        def load_scale_rows(queue, plane, scales):
+            passes = scales.shape[0]
+            for q in range(4):
+                queue.dma_start(
+                    plane[32 * q : 32 * q + 4, :].bitcast(I32).rearrange("r (a c) -> r a c", a=passes),
+                    scales[:, 4 * q : 4 * q + 4, :].bitcast(I32).rearrange("a r c -> r a c"),
+                )
+
+        def load_words(words, name):
+            tile = keep.tile([P, words.shape[1]], I32, name=name, align_bytes=64)
+            nc.sync.dma_start(tile[:], words.rearrange("p c i -> p (c i)").bitcast(I32))
+            return tile
+
+        def load_rows(rows, name, pieces):
+            width = rows.shape[1] // pieces
+            tiles = []
+            for c0 in range(0, rows.shape[1], width):
+                raw = keep.tile([P, PACK, width], F32, name="%s_%d" % (name, c0))
+                nc.sync.dma_start(raw[:], rows[:, c0 : c0 + width].rearrange("(p j) c -> p j c", j=PACK))
+                tiles.append(raw)
+            return tiles
+
+        def load_plain(src, name):
+            tile = keep.tile(list(src.shape), F32, name=name)
+            nc.sync.dma_start(tile[:], src)
+            return tile
+
+        tab_plane = keep.tile([P, 2 * T], U8, name="tab_plane", align_bytes=64)
+        nc.vector.memset(tab_plane[:, 0:T].bitcast(I32), 0)
+        nc.gpsimd.memset(tab_plane[:, T : 2 * T].bitcast(I32), 0)
+        w4_plane_in = zeroed_plane(2 * H, "w4_plane_in")
+        tab2_plane = zeroed_plane(T, "tab2_plane")
+        w8_plane = zeroed_plane(N, "w8_plane")
+
+        tab_sb = [load_words(tab_words[0], "tab_sb0")]
+        offs_sb = load_list(offs, "offs_sb")
+        load_scale_rows(nc.sync, tab_plane, tab_scales)
+        load_scale_rows(nc.gpsimd, w4_plane_in, w4_scales)
+        w4_in = keep.tile([P, 2 * 2 * H], U8, name="w4_in")
+        nc.sync.dma_start(
+            w4_in[:].bitcast(I32).rearrange("p (a c) -> p a c", a=2),
+            w4_words.bitcast(I32).rearrange("a p c -> p a c"),
+        )
+        wb_raw = [load_rows(wb[0:512, :], "wb_raw0", 1), load_rows(wb[512:1024, :], "wb_raw1", 1)]
+        tab_sb.append(load_words(tab_words[1], "tab_sb1"))
+        gain_sb = keep.tile([P, PACK], F32, name="gain_sb")
+        nc.sync.dma_start(gain_sb[:], gain.rearrange("(p t) -> p t", t=PACK))
+        wo1_raw = load_rows(wo1, "wo1_raw", 2)
+        offs2_sb = load_list(offs2, "offs2_sb")
+        tab2_sb = load_words(tab2_words[0], "tab2_sb")
+        load_scale_rows(nc.sync, tab2_plane, tab2_scales)
+        pages = [load_plain(page1[0:P, :], "page0")]
+        offs3_sb = load_list(offs3, "offs3_sb")
+        wg1_sb = [load_plain(wg1[:, 0:256], "wg1_sb0")]
+        pages.append(load_plain(page1[P : 2 * P, :], "page1"))
+        pages.append(load_plain(page1[2 * P : 3 * P, :], "page2"))
+        wc_raw = load_rows(wc, "wc_raw", 1)
+        wg1_sb.append(load_plain(wg1[:, 256:512], "wg1_sb1"))
+        pages.append(load_plain(page1[3 * P : 4 * P, :], "page3"))
+        pos1_sb = load_list(pos1, "pos1_sb")
+        wg1_sb.append(load_plain(wg1[:, 512:1024], "wg1_sb2"))
+        offs4_sb = load_list(offs4, "offs4_sb")
+        wg2_sb = load_plain(wg2, "wg2_sb")
+        w8_sb = load_words(w8_words[0], "w8_sb")
+        load_scale_rows(nc.sync, w8_plane, w8_scales)
+
+        def gather(dst, window, offsets):
+            nc.vector.tensor_copy(dst, window.indirect(offsets))
+
+        def quantize(values, width, name, tag, bufs):
+            codes = ring.tile([P, width], U32, name=name + "_codes", tag=tag + "_codes", bufs=bufs, align_bytes=64)
+            plane = ring.tile([P, width], U8, name=name + "_plane", tag=tag + "_plane", bufs=bufs, align_bytes=64)
+            nc.vector.quantize_mx(out=codes[:].bitcast(FP8X4), scales=plane[:], in_=values[:])
+            return codes, plane
+
+        def quantize_weight(raws, name, dealt, engines):
+            grouped = ring.tile([P, PACK * 512], BF16, name=name + "_grouped", tag="grouped", align_bytes=64)
+            order = "p (i m j) -> p m j i" if dealt else "p (m i j) -> p m j i"
+            dst = grouped[:].rearrange(order, i=4, j=PACK)
+            step = 128 // len(raws)
+            for piece, (raw, copy) in enumerate(zip(raws, engines)):
+                copy(dst[:, piece * step : (piece + 1) * step], raw[:].rearrange("p j (m i) -> p m j i", i=4))
+            return quantize(grouped, 512, name, name, 1)
+
+        def gather_tab(source, dtype, c0, c1, name, tag=None):
+            tile = keep.tile([P, c1 - c0], dtype, name=name, tag=tag or name, align_bytes=64)
+            gather(tile[:], source, offs_sb[:, c0 // 16 : c1 // 16])
+            return tile
+
+        half_list = S // 2
+        words0 = gather_tab(tab_sb[0][:].bitcast(U32), U32, 0, S, "v_words0")
+        plane0 = gather_tab(tab_plane[:, 0:T], U8, 0, S, "v_plane0")
+        plane1_low = gather_tab(tab_plane[:, T : 2 * T], U8, 0, half_list, "v_plane1_low")
+
+        w4_sb = keep.tile([P, 2 * 2 * H], U8, name="w4_sb", align_bytes=64)
+        nc.scalar.copy(
+            w4_sb[:].bitcast(U16).rearrange("p (a t m) -> p a t m", a=2, t=PACK),
+            w4_in[:].bitcast(U16).rearrange("p (a m t) -> p a t m", a=2, t=PACK),
+        )
+        w4_plane = keep.tile([P, 2 * H], U8, name="w4_plane", align_bytes=64)
+        nc.vector.tensor_copy(
+            w4_plane[:].rearrange("p (a t m) -> p a t m", a=2, t=PACK),
+            w4_plane_in[:].rearrange("p (a m t) -> p a t m", a=2, t=PACK),
+        )
+        wb_q = [quantize_weight(wb_raw[a], "wb%d" % a, True, [nc.scalar.copy] * 2) for a in range(2)]
+        first = LAYER_BLOCKS[0][1]
+        words1 = [gather_tab(tab_sb[1][:].bitcast(U32), U32, 0, first, "v_words1_first")[:]]
+        planes1 = [plane1_low[:, c0:c1] for c0, c1 in LAYER_BLOCKS[:2]]
+
+        minus_two_gain = keep.tile([P, PACK], F32, name="minus_two_gain")
+        nc.gpsimd.tensor_scalar(minus_two_gain[:], gain_sb[:], -2.0, 0.0, ALU.mult, ALU.add)
+
+        h1 = [keep.tile([P, S], F32, name="h1_%d" % t) for t in range(PACK)]
+
+        def stage_one(index):
+            c0, c1 = LAYER_BLOCKS[index]
+            width = c1 - c0
+            v_codes = (words0[:, c0:c1].bitcast(FP8X4), words1[index].bitcast(FP8X4))
+            v_planes = (plane0[:, c0:c1], planes1[index])
+            for t in range(PACK):
+                left = psum.tile([P, width], F32, name="left", tag="scalar_bank", bufs=4)
+                right = psum.tile([P, width], F32, name="right", tag="right", bufs=4)
+                for a in range(2):
+                    col = a * H + t * P
+                    nc.tensor.matmul_mx(
+                        out=left[:],
+                        lhsT=w4_sb[:, 2 * col : 2 * (col + P)].bitcast(FP4X4),
+                        lhsT_scale=w4_plane[:, col : col + P],
+                        rhs=v_codes[a],
+                        rhs_scale=v_planes[a],
+                        start=(a == 0), stop=(a == 1),
+                    )
+                for a in range(2):
+                    codes, plane = wb_q[a]
+                    nc.tensor.matmul_mx(
+                        out=right[:],
+                        lhsT=codes[:, t * P : (t + 1) * P].bitcast(FP8X4),
+                        lhsT_scale=plane[:, t * P : (t + 1) * P],
+                        rhs=v_codes[a],
+                        rhs_scale=v_planes[a],
+                        start=(a == 0), stop=(a == 1),
+                    )
+                left_sb = keep.tile([P, width], F32, name="left_sb", tag="left_sb%d_%d" % (min(index, 1), t), align_bytes=64)
+                nc.scalar.copy(left_sb[:], left[:])
+                nc.vector.tensor_tensor(h1[t][:, c0:c1], right[:], left_sb[:], ALU.mult)
+
+        def interleave_and_quantize(rows, width, tag):
+            woven = keep.tile([P, width * PACK], BF16, name="woven", tag=tag, align_bytes=64)
+            nc.scalar.copy(
+                woven[:].rearrange("p (c i t) -> p c t i", i=4, t=PACK),
+                rows[:].rearrange("p (t c i) -> p c t i", i=4, t=PACK),
+            )
+            return quantize(woven, width, "z", "z", 2)
+
+        def make_z1(index):
+            c0, c1 = LAYER_BLOCKS[index]
+            width = c1 - c0
+            rows = keep.tile([P, PACK * width], BF16, name="z_rows", tag="z_rows%d" % index)
+            for t in range(PACK):
+                if index == 0:
+                    tanh = keep.tile([P, width], F32, name="tanh", tag="tanh%d" % t, align_bytes=64)
+                else:
+                    tanh = ring.tile([P, width], F32, name="tanh", tag="act")
+                nc.scalar.activation(tanh[:], h1[t][:, c0:c1], ACT.Tanh)
+                nc.scalar.activation(rows[:, t * width : (t + 1) * width], tanh[:], ACT.Copy, scale=gain_sb[:, t : t + 1])
+            return interleave_and_quantize(rows, width, "woven%d" % min(index, 1))
+
+        def stage_two(n, weight, z, factors, offsets, late_tag=None):
+            (w_codes, w_plane), (z_codes, z_plane) = weight, z
+            width = z_plane.shape[1]
+            y = psum.tile([P, width], F32, name="y", tag="scalar_bank", bufs=4)
+            nc.tensor.matmul_mx(
+                out=y[:],
+                lhsT=w_codes[:, n * P : (n + 1) * P].bitcast(FP8X4),
+                lhsT_scale=w_plane[:, n * P : (n + 1) * P],
+                rhs=z_codes[:].bitcast(FP8X4),
+                rhs_scale=z_plane[:],
+                start=True, stop=True,
+            )
+            if late_tag is None:
+                y_sb = ring.tile([P, width], F32, name="y_sb", tag="y_sb", bufs=4)
+            else:
+                y_sb = keep.tile([P, width], F32, name="y_late", tag=late_tag)
+            nc.scalar.copy(y_sb[:], y[:])
+            nc.vector.tensor_tensor(pages[n][:].indirect(offsets), y_sb[:], factors[:], ALU.mult)
+
+        def place_layers(index, z, tiles, late_tag=None):
+            c0, c1 = LAYER_BLOCKS[index]
+            for n in tiles:
+                stage_two(n, wo1_q, z, wg1_sb[index], offs3_sb[:, c0 // 16 : c1 // 16], late_tag)
+
+        stage_one(0)
+        words1_rest = gather_tab(tab_sb[1][:].bitcast(U32), U32, first, S, "v_words1_rest", "left_sb0_3")
+        words1.extend([words1_rest[:, c0 - first : c1 - first] for c0, c1 in LAYER_BLOCKS[1:]])
+        z1_0 = make_z1(0)
+        planes1.append(gather_tab(tab_plane[:, T : 2 * T], U8, half_list, S, "v_plane1_high", "tanh1")[:])
+        wo1_q = quantize_weight(wo1_raw, "wo1", False, [nc.scalar.copy, nc.scalar.copy])
+
+        v2_words = keep.tile([P, C], U32, name="v2_words", tag="woven0", align_bytes=64)
+        v2_plane = keep.tile([P, C], U8, name="v2_plane", align_bytes=64)
+        gather(v2_words[:], tab2_sb[:].bitcast(U32), offs2_sb[:])
+        gather(v2_plane[:], tab2_plane[:], offs2_sb[:])
+
+        stage_one(1)
+        place_layers(0, z1_0, range(3))
+        stage_one(2)
+        z1_1 = make_z1(1)
+        place_layers(0, z1_0, [3], "z_rows1")
+        place_layers(1, z1_1, range(3))
+
+        wc_codes, wc_plane = quantize_weight(wc_raw, "wc", True, [nc.scalar.copy])
+        shifted = []
+        for t in range(PACK):
+            h2 = psum.tile([P, C], F32, name="h2", tag="right", bufs=4)
+            nc.tensor.matmul_mx(
+                out=h2[:],
+                lhsT=wc_codes[:, t * P : (t + 1) * P].bitcast(FP8X4),
+                lhsT_scale=wc_plane[:, t * P : (t + 1) * P],
+                rhs=v2_words[:].bitcast(FP8X4),
+                rhs_scale=v2_plane[:],
+                start=True, stop=True,
+            )
+            picked = ring.tile([P, C], F32, name="picked", tag="picked")
+            gather(picked[:], h1[t][:], pos1_sb[:])
+            arg = keep.tile([P, C], F32, name="arg%d" % t)
+            nc.vector.scalar_tensor_tensor(arg[:], h2[:], -0.5 * math.pi, picked[:], ALU.add, ALU.add)
+            shifted.append(arg)
+
+        z1_2 = make_z1(2)
+        place_layers(1, z1_1, [3], "z_rows2")
+        place_layers(2, z1_2, range(3))
+
+        rows = keep.tile([P, PACK * C], BF16, name="z_rows", tag="z_rows3")
+        for t in range(PACK):
+            half = ring.tile([P, C], F32, name="half", tag="act")
+            nc.scalar.activation(half[:], shifted[t][:], ACT.Sin, scale=0.5)
+            square = ring.tile([P, C], F32, name="square", tag="act")
+            nc.scalar.activation(square[:], half[:], ACT.Square)
+            nc.scalar.activation(
+                rows[:, t * C : (t + 1) * C], square[:], ACT.Identity,
+                scale=minus_two_gain[:, t : t + 1], bias=gain_sb[:, t : t + 1],
+            )
+        z2 = interleave_and_quantize(rows, C, "woven1")
+        place_layers(2, z1_2, [3], "z_rows3")
+        for n in range(N // P):
+            stage_two(n, (w8_sb, w8_plane), z2, wg2_sb, offs4_sb[:])
+            nc.sync.dma_start(out[n * P : (n + 1) * P, :], pages[n][:])

@@ -29,7 +29,6 @@ def tile_list_treaty_layer_pages_kernel(
     nc = tc.nc
     with ExitStack() as ctx:
         keep = ctx.enter_context(tc.tile_pool(name="keep", bufs=1))
-        ring = ctx.enter_context(tc.tile_pool(name="ring", bufs=2))
         psum = ctx.enter_context(tc.psum_pool(name="psum", bufs=2))
 
         def load_list(src, name):
@@ -59,7 +58,7 @@ def tile_list_treaty_layer_pages_kernel(
             width = rows.shape[1] // pieces
             tiles = []
             for c0 in range(0, rows.shape[1], width):
-                raw = keep.tile([P, PACK, width], F32, name="%s_%d" % (name, c0))
+                raw = keep.tile([P, PACK, width], F32, name="%s_%d" % (name, c0), align_bytes=64)
                 nc.sync.dma_start(raw[:], rows[:, c0 : c0 + width].rearrange("(p j) c -> p j c", j=PACK))
                 tiles.append(raw)
             return tiles
@@ -79,14 +78,15 @@ def tile_list_treaty_layer_pages_kernel(
         tab_sb = [load_words(tab_words[0], "tab_sb0")]
         offs_sb = load_list(offs, "offs_sb")
         load_scale_rows(nc.sync, tab_plane, tab_scales)
-        load_scale_rows(nc.gpsimd, w4_plane_in, w4_scales)
         w4_in = keep.tile([P, 2 * 2 * H], U8, name="w4_in")
         nc.sync.dma_start(
             w4_in[:].bitcast(I32).rearrange("p (a c) -> p a c", a=2),
             w4_words.bitcast(I32).rearrange("a p c -> p a c"),
         )
-        wb_raw = [load_rows(wb[0:512, :], "wb_raw0", 1), load_rows(wb[512:1024, :], "wb_raw1", 1)]
+        wb_raw = [load_rows(wb[0:512, :], "wb_raw0", 1)]
         tab_sb.append(load_words(tab_words[1], "tab_sb1"))
+        load_scale_rows(nc.sync, w4_plane_in, w4_scales)
+        wb_raw.append(load_rows(wb[512:1024, :], "wb_raw1", 2))
         gain_sb = keep.tile([P, PACK], F32, name="gain_sb")
         nc.sync.dma_start(gain_sb[:], gain.rearrange("(p t) -> p t", t=PACK))
         wo1_raw = load_rows(wo1, "wo1_raw", 2)
@@ -97,11 +97,11 @@ def tile_list_treaty_layer_pages_kernel(
         offs3_sb = load_list(offs3, "offs3_sb")
         wg1_sb = [load_plain(wg1[:, 0:256], "wg1_sb0")]
         pages.append(load_plain(page1[P : 2 * P, :], "page1"))
-        pages.append(load_plain(page1[2 * P : 3 * P, :], "page2"))
-        wc_raw = load_rows(wc, "wc_raw", 1)
-        wg1_sb.append(load_plain(wg1[:, 256:512], "wg1_sb1"))
-        pages.append(load_plain(page1[3 * P : 4 * P, :], "page3"))
         pos1_sb = load_list(pos1, "pos1_sb")
+        pages.append(load_plain(page1[2 * P : 3 * P, :], "page2"))
+        wg1_sb.append(load_plain(wg1[:, 256:512], "wg1_sb1"))
+        wc_raw = load_rows(wc, "wc_raw", 2)
+        pages.append(load_plain(page1[3 * P : 4 * P, :], "page3"))
         wg1_sb.append(load_plain(wg1[:, 512:1024], "wg1_sb2"))
         offs4_sb = load_list(offs4, "offs4_sb")
         wg2_sb = load_plain(wg2, "wg2_sb")
@@ -111,20 +111,28 @@ def tile_list_treaty_layer_pages_kernel(
         def gather(dst, window, offsets):
             nc.vector.tensor_copy(dst, window.indirect(offsets))
 
-        def quantize(values, width, name, tag, bufs):
-            codes = ring.tile([P, width], U32, name=name + "_codes", tag=tag + "_codes", bufs=bufs, align_bytes=64)
-            plane = ring.tile([P, width], U8, name=name + "_plane", tag=tag + "_plane", bufs=bufs, align_bytes=64)
+        def quantize(values, width, name, codes_tag=None):
+            codes = keep.tile([P, width], U32, name=name + "_codes", tag=codes_tag or name + "_codes", align_bytes=64)
+            plane = keep.tile([P, width], U8, name=name + "_plane", align_bytes=64)
             nc.vector.quantize_mx(out=codes[:].bitcast(FP8X4), scales=plane[:], in_=values[:])
             return codes, plane
 
-        def quantize_weight(raws, name, dealt, engines):
-            grouped = ring.tile([P, PACK * 512], BF16, name=name + "_grouped", tag="grouped", align_bytes=64)
+        def round_weight(grouped, raws, pieces, dealt):
             order = "p (i m j) -> p m j i" if dealt else "p (m i j) -> p m j i"
             dst = grouped[:].rearrange(order, i=4, j=PACK)
             step = 128 // len(raws)
-            for piece, (raw, copy) in enumerate(zip(raws, engines)):
-                copy(dst[:, piece * step : (piece + 1) * step], raw[:].rearrange("p j (m i) -> p m j i", i=4))
-            return quantize(grouped, 512, name, name, 1)
+            for piece in pieces:
+                nc.scalar.copy(
+                    dst[:, piece * step : (piece + 1) * step], raws[piece][:].rearrange("p j (m i) -> p m j i", i=4)
+                )
+
+        def staging(name, width, tag=None, dtype=F32):
+            return keep.tile([P, width], dtype, name=name, tag=tag or name, align_bytes=64)
+
+        def quantize_weight(raws, name, tag):
+            grouped = staging(name + "_grouped", PACK * H, tag, BF16)
+            round_weight(grouped, raws, range(len(raws)), True)
+            return quantize(grouped, H, name)
 
         def gather_tab(source, dtype, c0, c1, name, tag=None):
             tile = keep.tile([P, c1 - c0], dtype, name=name, tag=tag or name, align_bytes=64)
@@ -146,24 +154,25 @@ def tile_list_treaty_layer_pages_kernel(
             w4_plane[:].rearrange("p (a t m) -> p a t m", a=2, t=PACK),
             w4_plane_in[:].rearrange("p (a m t) -> p a t m", a=2, t=PACK),
         )
-        wb_q = [quantize_weight(wb_raw[a], "wb%d" % a, True, [nc.scalar.copy] * 2) for a in range(2)]
+        wb_q = [quantize_weight(wb_raw[a], "wb%d" % a, "grouped%d" % a) for a in range(2)]
         first = LAYER_BLOCKS[0][1]
         words1 = [gather_tab(tab_sb[1][:].bitcast(U32), U32, 0, first, "v_words1_first")[:]]
         planes1 = [plane1_low[:, c0:c1] for c0, c1 in LAYER_BLOCKS[:2]]
 
         minus_two_gain = keep.tile([P, PACK], F32, name="minus_two_gain")
-        nc.gpsimd.tensor_scalar(minus_two_gain[:], gain_sb[:], -2.0, 0.0, ALU.mult, ALU.add)
+        nc.scalar.activation(minus_two_gain[:], gain_sb[:], ACT.Copy, scale=-2.0)
 
         h1 = [keep.tile([P, S], F32, name="h1_%d" % t) for t in range(PACK)]
 
-        def stage_one(index):
+        def stage_one(index, tag):
             c0, c1 = LAYER_BLOCKS[index]
             width = c1 - c0
             v_codes = (words0[:, c0:c1].bitcast(FP8X4), words1[index].bitcast(FP8X4))
             v_planes = (plane0[:, c0:c1], planes1[index])
+            left_sb = staging("left_sb", PACK * width, tag)
             for t in range(PACK):
                 left = psum.tile([P, width], F32, name="left", tag="scalar_bank", bufs=4)
-                right = psum.tile([P, width], F32, name="right", tag="right", bufs=4)
+                right = psum.tile([P, width], F32, name="right", tag="vector_bank", bufs=4)
                 for a in range(2):
                     col = a * H + t * P
                     nc.tensor.matmul_mx(
@@ -184,35 +193,30 @@ def tile_list_treaty_layer_pages_kernel(
                         rhs_scale=v_planes[a],
                         start=(a == 0), stop=(a == 1),
                     )
-                left_sb = keep.tile([P, width], F32, name="left_sb", tag="left_sb%d_%d" % (min(index, 1), t), align_bytes=64)
-                nc.scalar.copy(left_sb[:], left[:])
-                nc.vector.tensor_tensor(h1[t][:, c0:c1], right[:], left_sb[:], ALU.mult)
+                nc.scalar.copy(left_sb[:, t * width : (t + 1) * width], left[:])
+                nc.vector.tensor_tensor(h1[t][:, c0:c1], right[:], left_sb[:, t * width : (t + 1) * width], ALU.mult)
 
-        def interleave_and_quantize(rows, width, tag):
-            woven = keep.tile([P, width * PACK], BF16, name="woven", tag=tag, align_bytes=64)
+        def weave_and_quantize(rows, width, tag, name, codes_tag=None):
+            woven = staging("woven", PACK * width, tag, BF16)
             nc.scalar.copy(
                 woven[:].rearrange("p (c i t) -> p c t i", i=4, t=PACK),
                 rows[:].rearrange("p (t c i) -> p c t i", i=4, t=PACK),
             )
-            return quantize(woven, width, "z", "z", 2)
+            return quantize(woven, width, name, codes_tag)
 
-        def make_z1(index):
+        def make_z1(index, tanh_slices, tag, codes_tag=None):
             c0, c1 = LAYER_BLOCKS[index]
             width = c1 - c0
-            rows = keep.tile([P, PACK * width], BF16, name="z_rows", tag="z_rows%d" % index)
+            rows = staging("z_rows", PACK * width, tag, BF16)
             for t in range(PACK):
-                if index == 0:
-                    tanh = keep.tile([P, width], F32, name="tanh", tag="tanh%d" % t, align_bytes=64)
-                else:
-                    tanh = ring.tile([P, width], F32, name="tanh", tag="act")
-                nc.scalar.activation(tanh[:], h1[t][:, c0:c1], ACT.Tanh)
-                nc.scalar.activation(rows[:, t * width : (t + 1) * width], tanh[:], ACT.Copy, scale=gain_sb[:, t : t + 1])
-            return interleave_and_quantize(rows, width, "woven%d" % min(index, 1))
+                tanh = tanh_slices[t % len(tanh_slices)]
+                nc.scalar.activation(tanh, h1[t][:, c0:c1], ACT.Tanh)
+                nc.scalar.activation(rows[:, t * width : (t + 1) * width], tanh, ACT.Copy, scale=gain_sb[:, t : t + 1])
+            return weave_and_quantize(rows, width, "woven%d" % index, "z1_%d" % index, codes_tag)
 
-        def stage_two(n, weight, z, factors, offsets, late_tag=None):
+        def stage_two(n, weight, z, factors, offsets, y_sb):
             (w_codes, w_plane), (z_codes, z_plane) = weight, z
-            width = z_plane.shape[1]
-            y = psum.tile([P, width], F32, name="y", tag="scalar_bank", bufs=4)
+            y = psum.tile([P, z_plane.shape[1]], F32, name="y", tag="scalar_bank", bufs=4)
             nc.tensor.matmul_mx(
                 out=y[:],
                 lhsT=w_codes[:, n * P : (n + 1) * P].bitcast(FP8X4),
@@ -221,41 +225,44 @@ def tile_list_treaty_layer_pages_kernel(
                 rhs_scale=z_plane[:],
                 start=True, stop=True,
             )
-            if late_tag is None:
-                y_sb = ring.tile([P, width], F32, name="y_sb", tag="y_sb", bufs=4)
-            else:
-                y_sb = keep.tile([P, width], F32, name="y_late", tag=late_tag)
-            nc.scalar.copy(y_sb[:], y[:])
-            nc.vector.tensor_tensor(pages[n][:].indirect(offsets), y_sb[:], factors[:], ALU.mult)
+            nc.scalar.copy(y_sb, y[:])
+            nc.vector.tensor_tensor(pages[n][:].indirect(offsets), y_sb, factors[:], ALU.mult)
 
-        def place_layers(index, z, tiles, late_tag=None):
+        def place_layers(index, z, tiles, y_slices):
             c0, c1 = LAYER_BLOCKS[index]
-            for n in tiles:
-                stage_two(n, wo1_q, z, wg1_sb[index], offs3_sb[:, c0 // 16 : c1 // 16], late_tag)
+            for n, y_sb in zip(tiles, y_slices):
+                stage_two(n, wo1_q, z, wg1_sb[index], offs3_sb[:, c0 // 16 : c1 // 16], y_sb)
 
-        stage_one(0)
-        words1_rest = gather_tab(tab_sb[1][:].bitcast(U32), U32, first, S, "v_words1_rest", "left_sb0_3")
+        def cut(tile, widths):
+            edges = [sum(widths[:i]) for i in range(len(widths) + 1)]
+            return [tile[:, a:b] for a, b in zip(edges, edges[1:])]
+
+        small, large = 256, 512
+        planes1.append(gather_tab(tab_plane[:, T : 2 * T], U8, half_list, S, "v_plane1_high", "grouped1")[:])
+        wo1_rounded = staging("wo1_grouped", PACK * N, "grouped0", BF16)
+        round_weight(wo1_rounded, wo1_raw, [0], False)
+        stage_one(0, "wo1_raw_0")
+        words1_rest = gather_tab(tab_sb[1][:].bitcast(U32), U32, first, S, "v_words1_rest", "wo1_raw_0")
         words1.extend([words1_rest[:, c0 - first : c1 - first] for c0, c1 in LAYER_BLOCKS[1:]])
-        z1_0 = make_z1(0)
-        planes1.append(gather_tab(tab_plane[:, T : 2 * T], U8, half_list, S, "v_plane1_high", "tanh1")[:])
-        wo1_q = quantize_weight(wo1_raw, "wo1", False, [nc.scalar.copy, nc.scalar.copy])
-
-        v2_words = keep.tile([P, C], U32, name="v2_words", tag="woven0", align_bytes=64)
-        v2_plane = keep.tile([P, C], U8, name="v2_plane", align_bytes=64)
-        gather(v2_words[:], tab2_sb[:].bitcast(U32), offs2_sb[:])
+        z1_0 = make_z1(0, cut(staging("tanh0", 4 * small), [small] * 4), "rows0")
+        round_weight(wo1_rounded, wo1_raw, [1], False)
+        v2_plane = staging("v2_plane", C, None, U8)
         gather(v2_plane[:], tab2_plane[:], offs2_sb[:])
+        wo1_q = quantize(wo1_rounded, N, "wo1", "tab2_plane")
 
-        stage_one(1)
-        place_layers(0, z1_0, range(3))
-        stage_one(2)
-        z1_1 = make_z1(1)
-        place_layers(0, z1_0, [3], "z_rows1")
-        place_layers(1, z1_1, range(3))
+        stage_one(1, "rows0")
+        v2_words = staging("v2_words", C, "rows0", U32)
+        gather(v2_words[:], tab2_sb[:].bitcast(U32), offs2_sb[:])
+        place_layers(0, z1_0, range(3), cut(staging("y0", 2 * small), [small] * 2) + [staging("y0_late", small)[:]])
+        wc_codes, wc_plane = quantize_weight(wc_raw, "wc", "grouped0")
+        stage_one(2, "wc_raw_256")
+        z1_1 = make_z1(1, cut(staging("tanh1", 4 * small, "tab_sb0"), [small] * 4), "rows1", "y0")
+        late0, tanh_a, tanh_b, *h2_sb = cut(staging("after1", small + 6 * large, "rows1"), [small] + [large] * 6)
+        place_layers(0, z1_0, [3], [late0])
 
-        wc_codes, wc_plane = quantize_weight(wc_raw, "wc", True, [nc.scalar.copy])
-        shifted = []
+        shifted = cut(staging("shifted", PACK * C, "woven1"), [C] * PACK)
         for t in range(PACK):
-            h2 = psum.tile([P, C], F32, name="h2", tag="right", bufs=4)
+            h2 = psum.tile([P, C], F32, name="h2", tag="vector_bank", bufs=4)
             nc.tensor.matmul_mx(
                 out=h2[:],
                 lhsT=wc_codes[:, t * P : (t + 1) * P].bitcast(FP8X4),
@@ -264,28 +271,33 @@ def tile_list_treaty_layer_pages_kernel(
                 rhs_scale=v2_plane[:],
                 start=True, stop=True,
             )
-            picked = ring.tile([P, C], F32, name="picked", tag="picked")
-            gather(picked[:], h1[t][:], pos1_sb[:])
-            arg = keep.tile([P, C], F32, name="arg%d" % t)
-            nc.vector.scalar_tensor_tensor(arg[:], h2[:], -0.5 * math.pi, picked[:], ALU.add, ALU.add)
-            shifted.append(arg)
+            nc.scalar.activation(h2_sb[t], h2[:], ACT.Copy, bias=-0.5 * math.pi)
+            nc.vector.tensor_tensor(shifted[t], h1[t][:].indirect(pos1_sb[:]), h2_sb[t], ALU.add)
 
-        z1_2 = make_z1(2)
-        place_layers(1, z1_1, [3], "z_rows2")
-        place_layers(2, z1_2, range(3))
+        place_layers(1, z1_1, range(3), cut(staging("y1", 3 * small), [small] * 3))
+        z1_2 = make_z1(2, [tanh_a, tanh_b], "rows2")
+        late1, half_a, half_b = cut(staging("after2", small + 2 * large, "rows2"), [small, large, large])
+        place_layers(1, z1_1, [3], [late1])
 
-        rows = keep.tile([P, PACK * C], BF16, name="z_rows", tag="z_rows3")
-        for t in range(PACK):
-            half = ring.tile([P, C], F32, name="half", tag="act")
-            nc.scalar.activation(half[:], shifted[t][:], ACT.Sin, scale=0.5)
-            square = ring.tile([P, C], F32, name="square", tag="act")
-            nc.scalar.activation(square[:], half[:], ACT.Square)
+        rows = staging("z_rows", PACK * C, "rows3", BF16)
+
+        def make_z2_rows(t, square):
+            half = (half_a, half_b)[t % 2]
+            nc.scalar.activation(half, shifted[t], ACT.Sin, scale=0.5)
+            nc.scalar.activation(square[:], half, ACT.Square)
             nc.scalar.activation(
                 rows[:, t * C : (t + 1) * C], square[:], ACT.Identity,
                 scale=minus_two_gain[:, t : t + 1], bias=gain_sb[:, t : t + 1],
             )
-        z2 = interleave_and_quantize(rows, C, "woven1")
-        place_layers(2, z1_2, [3], "z_rows3")
+
+        make_z2_rows(0, staging("square0", C))
+        place_layers(2, z1_2, range(3), cut(staging("y2", 3 * large, "wb_raw0_0"), [large] * 3))
+        make_z2_rows(1, staging("square1", C, "wb_raw1_0"))
+        make_z2_rows(2, staging("square2", C, "square0"))
+        make_z2_rows(3, staging("square3", C, "wo1_raw_256"))
+        z2 = weave_and_quantize(rows, C, "woven2", "z2")
+        place_layers(2, z1_2, [3], [staging("late2", large, "rows3")[:]])
+        y_last = cut(staging("y3", 4 * large, "tab_sb1"), [large] * 4)
         for n in range(N // P):
-            stage_two(n, (w8_sb, w8_plane), z2, wg2_sb, offs4_sb[:])
+            stage_two(n, (w8_sb, w8_plane), z2, wg2_sb, offs4_sb[:], y_last[n])
             nc.sync.dma_start(out[n * P : (n + 1) * P, :], pages[n][:])

@@ -20,6 +20,10 @@ PACK = 4
 FLOPS = 2 * (2 * K * H * S + K2 * H * C + H * N * (S + C))
 
 LAYER_BLOCKS = ((0, 256), (256, 512), (512, 1024))
+WB_SCALAR_SHARE = (4, 2)
+BLOCK = 256
+LAYER_Z = S // BLOCK
+LAST_ORDER = ((4, 0), (4, 1), (5, 0), (5, 1), (4, 2), (5, 2), (4, 3), (5, 3))
 
 
 def tile_list_treaty_layer_pages_kernel(
@@ -29,6 +33,8 @@ def tile_list_treaty_layer_pages_kernel(
     nc = tc.nc
     with ExitStack() as ctx:
         keep = ctx.enter_context(tc.tile_pool(name="keep", bufs=1))
+        y0_bytes = ctx.enter_context(tc.tile_pool(name="y0_bytes", bufs=1))
+        wo1_bytes = ctx.enter_context(tc.tile_pool(name="wo1_bytes", bufs=1))
         psum = ctx.enter_context(tc.psum_pool(name="psum", bufs=2))
 
         def load_list(src, name):
@@ -49,131 +55,135 @@ def tile_list_treaty_layer_pages_kernel(
                     scales[:, 4 * q : 4 * q + 4, :].bitcast(I32).rearrange("a r c -> r a c"),
                 )
 
-        def load_words(words, name):
-            tile = keep.tile([P, words.shape[1]], I32, name=name, align_bytes=64)
+        def load_words(words, tile):
             nc.sync.dma_start(tile[:], words.rearrange("p c i -> p (c i)").bitcast(I32))
             return tile
 
-        def load_rows(rows, name, pieces):
-            width = rows.shape[1] // pieces
-            tiles = []
-            for c0 in range(0, rows.shape[1], width):
-                raw = keep.tile([P, PACK, width], F32, name="%s_%d" % (name, c0), align_bytes=64)
-                nc.sync.dma_start(raw[:], rows[:, c0 : c0 + width].rearrange("(p j) c -> p j c", j=PACK))
-                tiles.append(raw)
-            return tiles
+        def staging(name, width, tag=None, dtype=F32):
+            return keep.tile([P, width], dtype, name=name, tag=tag or name, align_bytes=64)
+
+        def load_rows(rows, raw):
+            nc.sync.dma_start(raw[:], rows.rearrange("(p j) c -> p j c", j=PACK))
+            return raw
 
         def load_plain(src, name):
             tile = keep.tile(list(src.shape), F32, name=name)
             nc.sync.dma_start(tile[:], src)
             return tile
 
-        tab_plane = keep.tile([P, 2 * T], U8, name="tab_plane", align_bytes=64)
-        nc.vector.memset(tab_plane[:, 0:T].bitcast(I32), 0)
-        nc.gpsimd.memset(tab_plane[:, T : 2 * T].bitcast(I32), 0)
+        tab_plane = zeroed_plane(T, "tab_plane")
+        plane1 = keep.tile([P, S], U8, name="v_plane1", align_bytes=64)
+        nc.gpsimd.memset(plane1[:].bitcast(I32), 0)
         w4_plane_in = zeroed_plane(2 * H, "w4_plane_in")
         tab2_plane = zeroed_plane(T, "tab2_plane")
         w8_plane = zeroed_plane(N, "w8_plane")
 
-        tab_sb = [load_words(tab_words[0], "tab_sb0")]
+        tab_sb = [load_words(tab_words[0], staging("tab_sb0", T, None, I32))]
         offs_sb = load_list(offs, "offs_sb")
-        load_scale_rows(nc.sync, tab_plane, tab_scales)
+        for q in range(4):
+            nc.sync.dma_start(
+                tab_plane[32 * q : 32 * q + 8, :].bitcast(I32), tab_scales[:, 4 * q : 4 * q + 4, :].bitcast(I32)
+            )
+        tab_sb.append(load_words(tab_words[1], staging("tab_sb1", T, None, I32)))
         w4_in = keep.tile([P, 2 * 2 * H], U8, name="w4_in")
         nc.sync.dma_start(
             w4_in[:].bitcast(I32).rearrange("p (a c) -> p a c", a=2),
             w4_words.bitcast(I32).rearrange("a p c -> p a c"),
         )
-        wb_raw = [load_rows(wb[0:512, :], "wb_raw0", 1)]
-        tab_sb.append(load_words(tab_words[1], "tab_sb1"))
+        wb_raw = [load_rows(wb[0:512, :], keep.tile([P, PACK, H], F32, name="wb_raw0", align_bytes=64))]
         load_scale_rows(nc.sync, w4_plane_in, w4_scales)
-        wb_raw.append(load_rows(wb[512:1024, :], "wb_raw1", 2))
-        gain_sb = keep.tile([P, PACK], F32, name="gain_sb")
-        nc.sync.dma_start(gain_sb[:], gain.rearrange("(p t) -> p t", t=PACK))
-        wo1_raw = load_rows(wo1, "wo1_raw", 2)
-        offs2_sb = load_list(offs2, "offs2_sb")
-        tab2_sb = load_words(tab2_words[0], "tab2_sb")
-        load_scale_rows(nc.sync, tab2_plane, tab2_scales)
-        pages = [load_plain(page1[0:P, :], "page0")]
-        offs3_sb = load_list(offs3, "offs3_sb")
-        wg1_sb = [load_plain(wg1[:, 0:256], "wg1_sb0")]
-        pages.append(load_plain(page1[P : 2 * P, :], "page1"))
-        pos1_sb = load_list(pos1, "pos1_sb")
-        pages.append(load_plain(page1[2 * P : 3 * P, :], "page2"))
-        wg1_sb.append(load_plain(wg1[:, 256:512], "wg1_sb1"))
-        wc_raw = load_rows(wc, "wc_raw", 2)
-        pages.append(load_plain(page1[3 * P : 4 * P, :], "page3"))
-        wg1_sb.append(load_plain(wg1[:, 512:1024], "wg1_sb2"))
-        offs4_sb = load_list(offs4, "offs4_sb")
-        wg2_sb = load_plain(wg2, "wg2_sb")
-        w8_sb = load_words(w8_words[0], "w8_sb")
-        load_scale_rows(nc.sync, w8_plane, w8_scales)
+        wb_raw.append(load_rows(wb[512:1024, :], keep.tile([P, PACK, H], F32, name="wb_raw1", align_bytes=64)))
 
         def gather(dst, window, offsets):
             nc.vector.tensor_copy(dst, window.indirect(offsets))
 
-        def quantize(values, width, name, codes_tag=None):
-            codes = keep.tile([P, width], U32, name=name + "_codes", tag=codes_tag or name + "_codes", align_bytes=64)
+        def quantize(values, codes, name):
+            width = codes.shape[1]
             plane = keep.tile([P, width], U8, name=name + "_plane", align_bytes=64)
             nc.vector.quantize_mx(out=codes[:].bitcast(FP8X4), scales=plane[:], in_=values[:])
             return codes, plane
 
-        def round_weight(grouped, raws, pieces, dealt):
-            order = "p (i m j) -> p m j i" if dealt else "p (m i j) -> p m j i"
-            dst = grouped[:].rearrange(order, i=4, j=PACK)
-            step = 128 // len(raws)
-            for piece in pieces:
-                nc.scalar.copy(
-                    dst[:, piece * step : (piece + 1) * step], raws[piece][:].rearrange("p j (m i) -> p m j i", i=4)
-                )
+        def round_dealt(copy, grouped, raw, t0, t1):
+            copy(
+                grouped[:, t0 * H : t1 * H].rearrange("p (t m j) -> p m j t", t=t1 - t0, j=PACK),
+                raw[:].rearrange("p j (m t) -> p m j t", t=PACK)[:, :, :, t0:t1],
+            )
 
-        def staging(name, width, tag=None, dtype=F32):
-            return keep.tile([P, width], dtype, name=name, tag=tag or name, align_bytes=64)
-
-        def quantize_weight(raws, name, tag):
+        def quantize_weight(raw, name, tag, shares, codes_tag=None):
             grouped = staging(name + "_grouped", PACK * H, tag, BF16)
-            round_weight(grouped, raws, range(len(raws)), True)
-            return quantize(grouped, H, name)
+            for copy, t0, t1 in shares:
+                round_dealt(copy, grouped, raw, t0, t1)
+            return quantize(grouped, staging(name + "_codes", H, codes_tag, U32), name)
 
         def gather_tab(source, dtype, c0, c1, name, tag=None):
             tile = keep.tile([P, c1 - c0], dtype, name=name, tag=tag or name, align_bytes=64)
             gather(tile[:], source, offs_sb[:, c0 // 16 : c1 // 16])
             return tile
 
-        half_list = S // 2
         words0 = gather_tab(tab_sb[0][:].bitcast(U32), U32, 0, S, "v_words0")
-        plane0 = gather_tab(tab_plane[:, 0:T], U8, 0, S, "v_plane0")
-        plane1_low = gather_tab(tab_plane[:, T : 2 * T], U8, 0, half_list, "v_plane1_low")
+        plane0 = gather_tab(tab_plane[:], U8, 0, S, "v_plane0")
+        nc.sync.dma_start(plane1[0:100, :].bitcast(I32), plane0[4:104, :].bitcast(I32))
+
+        gain_sb = keep.tile([P, PACK], F32, name="gain_sb")
+        nc.sync.dma_start(gain_sb[:], gain.rearrange("(p t) -> p t", t=PACK))
+        wo1_raw = load_rows(wo1, keep.tile([P, PACK, N], F32, name="wo1_raw", align_bytes=64))
+        offs2_sb = load_list(offs2, "offs2_sb")
+        load_scale_rows(nc.sync, tab2_plane, tab2_scales)
+        pages = [load_plain(page1[0:P, :], "page0")]
+        offs3_sb = load_list(offs3, "offs3_sb")
+        wg1_sb = [load_plain(wg1[:, 0:256], "wg1_sb0")[:]]
+        pages.append(load_plain(page1[P : 2 * P, :], "page1"))
+        pos1_sb = load_list(pos1, "pos1_sb")
+        pages.append(load_plain(page1[2 * P : 3 * P, :], "page2"))
+        wg1_sb.append(load_plain(wg1[:, 256:512], "wg1_sb1")[:])
+        tab2_sb = load_words(tab2_words[0], staging("tab2_sb", T, None, I32))
+        pages.append(load_plain(page1[3 * P : 4 * P, :], "page3"))
+        wc_raw = load_rows(wc, keep.tile([P, PACK, H], F32, name="wc_raw", align_bytes=64))
+        wg1_high = load_plain(wg1[:, 512:1024], "wg1_sb2")
+        wg1_sb.extend([wg1_high[:, 0:BLOCK], wg1_high[:, BLOCK : 2 * BLOCK]])
+        offs4_sb = load_list(offs4, "offs4_sb")
+        wg2_all = load_plain(wg2, "wg2_sb")
+        wg2_sb = [wg2_all[:, 0:BLOCK], wg2_all[:, BLOCK : 2 * BLOCK]]
+        w8_sb = load_words(w8_words[0], staging("w8_sb", N, None, I32))
+        load_scale_rows(nc.sync, w8_plane, w8_scales)
 
         w4_sb = keep.tile([P, 2 * 2 * H], U8, name="w4_sb", align_bytes=64)
         nc.scalar.copy(
-            w4_sb[:].bitcast(U16).rearrange("p (a t m) -> p a t m", a=2, t=PACK),
-            w4_in[:].bitcast(U16).rearrange("p (a m t) -> p a t m", a=2, t=PACK),
+            w4_sb[:].bitcast(U16).rearrange("p (a t m) -> p a m t", a=2, t=PACK),
+            w4_in[:].bitcast(U16).rearrange("p (a m t) -> p a m t", a=2, t=PACK),
         )
         w4_plane = keep.tile([P, 2 * H], U8, name="w4_plane", align_bytes=64)
         nc.vector.tensor_copy(
             w4_plane[:].rearrange("p (a t m) -> p a t m", a=2, t=PACK),
             w4_plane_in[:].rearrange("p (a m t) -> p a t m", a=2, t=PACK),
         )
-        wb_q = [quantize_weight(wb_raw[a], "wb%d" % a, "grouped%d" % a) for a in range(2)]
-        first = LAYER_BLOCKS[0][1]
-        words1 = [gather_tab(tab_sb[1][:].bitcast(U32), U32, 0, first, "v_words1_first")[:]]
-        planes1 = [plane1_low[:, c0:c1] for c0, c1 in LAYER_BLOCKS[:2]]
+        words1 = {}
+        for index in (0, 2):
+            c0, c1 = LAYER_BLOCKS[index]
+            words1[index] = gather_tab(tab_sb[1][:].bitcast(U32), U32, c0, c1, "v_words1_%d" % index)[:]
+        on_scalar = [(nc.scalar.copy, 0, PACK)]
+        wb_q = [
+            quantize_weight(wb_raw[a], "wb%d" % a, "grouped%d" % a, [(nc.scalar.copy, 0, t), (nc.vector.tensor_copy, t, PACK)][: 1 if t == PACK else 2])
+            for a, t in enumerate(WB_SCALAR_SHARE)
+        ]
+        words1[1] = gather_tab(tab_sb[1][:].bitcast(U32), U32, *LAYER_BLOCKS[1], "v_words1_1", "grouped1")[:]
 
         minus_two_gain = keep.tile([P, PACK], F32, name="minus_two_gain")
         nc.scalar.activation(minus_two_gain[:], gain_sb[:], ACT.Copy, scale=-2.0)
 
         h1 = [keep.tile([P, S], F32, name="h1_%d" % t) for t in range(PACK)]
 
-        def stage_one(index, tag):
+        def stage_one(index, left_sb):
             c0, c1 = LAYER_BLOCKS[index]
             width = c1 - c0
+            passes = (1, 0) if index == 1 else (0, 1)
             v_codes = (words0[:, c0:c1].bitcast(FP8X4), words1[index].bitcast(FP8X4))
-            v_planes = (plane0[:, c0:c1], planes1[index])
-            left_sb = staging("left_sb", PACK * width, tag)
+            v_planes = (plane0[:, c0:c1], plane1[:, c0:c1])
+            v_planes_packed = (plane0[:, c0:c1], plane0[4:P, c0:c1])
             for t in range(PACK):
                 left = psum.tile([P, width], F32, name="left", tag="scalar_bank", bufs=4)
                 right = psum.tile([P, width], F32, name="right", tag="vector_bank", bufs=4)
-                for a in range(2):
+                for a in passes:
                     col = a * H + t * P
                     nc.tensor.matmul_mx(
                         out=left[:],
@@ -181,42 +191,60 @@ def tile_list_treaty_layer_pages_kernel(
                         lhsT_scale=w4_plane[:, col : col + P],
                         rhs=v_codes[a],
                         rhs_scale=v_planes[a],
-                        start=(a == 0), stop=(a == 1),
+                        start=(a == passes[0]), stop=(a == passes[1]),
                     )
-                for a in range(2):
+                for a in passes:
                     codes, plane = wb_q[a]
                     nc.tensor.matmul_mx(
                         out=right[:],
                         lhsT=codes[:, t * P : (t + 1) * P].bitcast(FP8X4),
                         lhsT_scale=plane[:, t * P : (t + 1) * P],
                         rhs=v_codes[a],
-                        rhs_scale=v_planes[a],
-                        start=(a == 0), stop=(a == 1),
+                        rhs_scale=v_planes_packed[a],
+                        start=(a == passes[0]), stop=(a == passes[1]),
                     )
                 nc.scalar.copy(left_sb[:, t * width : (t + 1) * width], left[:])
                 nc.vector.tensor_tensor(h1[t][:, c0:c1], right[:], left_sb[:, t * width : (t + 1) * width], ALU.mult)
 
-        def weave_and_quantize(rows, width, tag, name, codes_tag=None):
+        def weave_and_quantize(rows, width, tag, name, codes):
             woven = staging("woven", PACK * width, tag, BF16)
             nc.scalar.copy(
                 woven[:].rearrange("p (c i t) -> p c t i", i=4, t=PACK),
                 rows[:].rearrange("p (t c i) -> p c t i", i=4, t=PACK),
             )
-            return quantize(woven, width, name, codes_tag)
+            return quantize(woven, codes, name)
 
-        def make_z1(index, tanh_slices, tag, codes_tag=None):
-            c0, c1 = LAYER_BLOCKS[index]
-            width = c1 - c0
-            rows = staging("z_rows", PACK * width, tag, BF16)
+        def make_z1(index, tanh_slices, codes, rows=None):
+            c0 = index * BLOCK
+            if rows is None:
+                rows = staging("z_rows", PACK * BLOCK, "rows%d" % index, BF16)
             for t in range(PACK):
-                tanh = tanh_slices[t % len(tanh_slices)]
-                nc.scalar.activation(tanh, h1[t][:, c0:c1], ACT.Tanh)
-                nc.scalar.activation(rows[:, t * width : (t + 1) * width], tanh, ACT.Copy, scale=gain_sb[:, t : t + 1])
-            return weave_and_quantize(rows, width, "woven%d" % index, "z1_%d" % index, codes_tag)
+                nc.scalar.activation(tanh_slices[t], h1[t][:, c0 : c0 + BLOCK], ACT.Tanh)
+                nc.scalar.activation(
+                    rows[:, t * BLOCK : (t + 1) * BLOCK], tanh_slices[t], ACT.Copy, scale=gain_sb[:, t : t + 1]
+                )
+            return weave_and_quantize(rows, BLOCK, "woven%d" % index, "z%d" % index, codes)
 
-        def stage_two(n, weight, z, factors, offsets, y_sb):
-            (w_codes, w_plane), (z_codes, z_plane) = weight, z
-            y = psum.tile([P, z_plane.shape[1]], F32, name="y", tag="scalar_bank", bufs=4)
+        def make_z2(index, half_slices):
+            c0 = (index - LAYER_Z) * BLOCK
+            rows = staging("z_rows", PACK * BLOCK, "rows%d" % index, BF16)
+            squares = cut(staging("squares", PACK * BLOCK, ("wb_raw1", "wo1_raw")[index - LAYER_Z]))
+            for t in range(PACK):
+                nc.scalar.activation(half_slices[t], shifted[t][:, c0 : c0 + BLOCK], ACT.Sin, scale=0.5)
+                nc.scalar.activation(squares[t], half_slices[t], ACT.Square)
+                nc.scalar.activation(
+                    rows[:, t * BLOCK : (t + 1) * BLOCK], squares[t], ACT.Identity,
+                    scale=minus_two_gain[:, t : t + 1], bias=gain_sb[:, t : t + 1],
+                )
+            return weave_and_quantize(rows, BLOCK, "woven%d" % index, "z%d" % index, staging("z%d_codes" % index, BLOCK, None, U32))
+
+        def place(index, n, y_sb):
+            if index < LAYER_Z:
+                (w_codes, w_plane), factors, offsets, c0 = wo1_q, wg1_sb[index], offs3_sb, index * BLOCK
+            else:
+                (w_codes, w_plane), factors, offsets, c0 = (w8_sb, w8_plane), wg2_sb[index - LAYER_Z], offs4_sb, (index - LAYER_Z) * BLOCK
+            z_codes, z_plane = z[index]
+            y = psum.tile([P, BLOCK], F32, name="y", tag="scalar_bank", bufs=4)
             nc.tensor.matmul_mx(
                 out=y[:],
                 lhsT=w_codes[:, n * P : (n + 1) * P].bitcast(FP8X4),
@@ -226,41 +254,45 @@ def tile_list_treaty_layer_pages_kernel(
                 start=True, stop=True,
             )
             nc.scalar.copy(y_sb, y[:])
-            nc.vector.tensor_tensor(pages[n][:].indirect(offsets), y_sb, factors[:], ALU.mult)
+            window = pages[n][:].indirect(offsets[:, c0 // 16 : (c0 + BLOCK) // 16])
+            nc.vector.tensor_tensor(window, y_sb, factors, ALU.mult)
 
-        def place_layers(index, z, tiles, y_slices):
-            c0, c1 = LAYER_BLOCKS[index]
-            for n, y_sb in zip(tiles, y_slices):
-                stage_two(n, wo1_q, z, wg1_sb[index], offs3_sb[:, c0 // 16 : c1 // 16], y_sb)
+        def cut(tile, width=BLOCK):
+            return [tile[:, c0 : c0 + width] for c0 in range(0, tile.shape[1], width)]
 
-        def cut(tile, widths):
-            edges = [sum(widths[:i]) for i in range(len(widths) + 1)]
-            return [tile[:, a:b] for a, b in zip(edges, edges[1:])]
-
-        small, large = 256, 512
-        planes1.append(gather_tab(tab_plane[:, T : 2 * T], U8, half_list, S, "v_plane1_high", "grouped1")[:])
-        wo1_rounded = staging("wo1_grouped", PACK * N, "grouped0", BF16)
-        round_weight(wo1_rounded, wo1_raw, [0], False)
-        stage_one(0, "wo1_raw_0")
-        words1_rest = gather_tab(tab_sb[1][:].bitcast(U32), U32, first, S, "v_words1_rest", "wo1_raw_0")
-        words1.extend([words1_rest[:, c0 - first : c1 - first] for c0, c1 in LAYER_BLOCKS[1:]])
-        z1_0 = make_z1(0, cut(staging("tanh0", 4 * small), [small] * 4), "rows0")
-        round_weight(wo1_rounded, wo1_raw, [1], False)
+        stage_one(0, staging("left0", PACK * BLOCK))
+        wo1_rounded = wo1_bytes.tile([P, PACK * N], BF16, name="wo1_rounded", align_bytes=64, offset=0)
+        nc.vector.tensor_copy(
+            wo1_rounded[:].rearrange("p (m i j) -> p m j i", i=4, j=PACK),
+            wo1_raw[:].rearrange("p j (m i) -> p m j i", i=4),
+        )
         v2_plane = staging("v2_plane", C, None, U8)
         gather(v2_plane[:], tab2_plane[:], offs2_sb[:])
-        wo1_q = quantize(wo1_rounded, N, "wo1", "tab2_plane")
+        wo1_q = quantize(wo1_rounded, staging("wo1_codes", N, "tab2_plane", U32), "wo1")
+        rows0 = wo1_bytes.tile([P, PACK * BLOCK], BF16, name="rows0", align_bytes=64, offset=16 * BLOCK)
+        z0_codes = wo1_bytes.tile([P, BLOCK], U32, name="z0_codes", align_bytes=64, offset=0)
+        z = [make_z1(0, cut(staging("tanh0", PACK * BLOCK)), z0_codes, rows0)]
 
-        stage_one(1, "rows0")
-        v2_words = staging("v2_words", C, "rows0", U32)
+        stage_one(1, wo1_bytes.tile([P, PACK * BLOCK], F32, name="left1", align_bytes=64, offset=4 * BLOCK))
+        y0 = y0_bytes.tile([P, 3 * BLOCK], F32, name="y0", align_bytes=64, offset=0)
+        for n, y_sb in enumerate(cut(y0) + cut(staging("y0_last", BLOCK))):
+            place(0, n, y_sb)
+        z1_codes = y0_bytes.tile([P, BLOCK], U32, name="z1_codes", align_bytes=64, offset=0)
+        z.append(make_z1(1, cut(staging("tanh1", PACK * BLOCK, "tab_sb0")), z1_codes))
+        stage_one(2, y0_bytes.tile([P, PACK * 2 * BLOCK], F32, name="left2", align_bytes=64, offset=4 * BLOCK))
+        for n, y_sb in enumerate(cut(staging("y1", 2 * BLOCK))):
+            place(1, n, y_sb)
+        v2_words = staging("v2_words", C, None, U32)
         gather(v2_words[:], tab2_sb[:].bitcast(U32), offs2_sb[:])
-        place_layers(0, z1_0, range(3), cut(staging("y0", 2 * small), [small] * 2) + [staging("y0_late", small)[:]])
-        wc_codes, wc_plane = quantize_weight(wc_raw, "wc", "grouped0")
-        stage_one(2, "wc_raw_256")
-        z1_1 = make_z1(1, cut(staging("tanh1", 4 * small, "tab_sb0"), [small] * 4), "rows1", "y0")
-        late0, tanh_a, tanh_b, *h2_sb = cut(staging("after1", small + 6 * large, "rows1"), [small] + [large] * 6)
-        place_layers(0, z1_0, [3], [late0])
-
-        shifted = cut(staging("shifted", PACK * C, "woven1"), [C] * PACK)
+        z.append(make_z1(2, cut(staging("tanh2", PACK * BLOCK, "rows1")), staging("z2_codes", BLOCK, None, U32)))
+        place(1, 2, staging("after2", BLOCK, "rows2")[:])
+        wc_codes, wc_plane = quantize_weight(wc_raw, "wc", "grouped0", on_scalar)
+        after_wc = cut(staging("after_wc", (1 + PACK) * BLOCK, "wc_raw"))
+        place(1, 3, after_wc[0])
+        z.append(make_z1(3, after_wc[1:], staging("z3_codes", BLOCK, None, U32)))
+        after3 = staging("after3", 2 * PACK * BLOCK + PACK * C, "rows3")
+        h2_sb = cut(after3[:, 2 * PACK * BLOCK :], C)
+        shifted = cut(staging("shifted", PACK * C, "woven1"), C)
         for t in range(PACK):
             h2 = psum.tile([P, C], F32, name="h2", tag="vector_bank", bufs=4)
             nc.tensor.matmul_mx(
@@ -274,30 +306,16 @@ def tile_list_treaty_layer_pages_kernel(
             nc.scalar.activation(h2_sb[t], h2[:], ACT.Copy, bias=-0.5 * math.pi)
             nc.vector.tensor_tensor(shifted[t], h1[t][:].indirect(pos1_sb[:]), h2_sb[t], ALU.add)
 
-        place_layers(1, z1_1, range(3), cut(staging("y1", 3 * small), [small] * 3))
-        z1_2 = make_z1(2, [tanh_a, tanh_b], "rows2")
-        late1, half_a, half_b = cut(staging("after2", small + 2 * large, "rows2"), [small, large, large])
-        place_layers(1, z1_1, [3], [late1])
-
-        rows = staging("z_rows", PACK * C, "rows3", BF16)
-
-        def make_z2_rows(t, square):
-            half = (half_a, half_b)[t % 2]
-            nc.scalar.activation(half, shifted[t], ACT.Sin, scale=0.5)
-            nc.scalar.activation(square[:], half, ACT.Square)
-            nc.scalar.activation(
-                rows[:, t * C : (t + 1) * C], square[:], ACT.Identity,
-                scale=minus_two_gain[:, t : t + 1], bias=gain_sb[:, t : t + 1],
-            )
-
-        make_z2_rows(0, staging("square0", C))
-        place_layers(2, z1_2, range(3), cut(staging("y2", 3 * large, "wb_raw0_0"), [large] * 3))
-        make_z2_rows(1, staging("square1", C, "wb_raw1_0"))
-        make_z2_rows(2, staging("square2", C, "square0"))
-        make_z2_rows(3, staging("square3", C, "wo1_raw_256"))
-        z2 = weave_and_quantize(rows, C, "woven2", "z2")
-        place_layers(2, z1_2, [3], [staging("late2", large, "rows3")[:]])
-        y_last = cut(staging("y3", 4 * large, "tab_sb1"), [large] * 4)
-        for n in range(N // P):
-            stage_two(n, (w8_sb, w8_plane), z2, wg2_sb, offs4_sb[:], y_last[n])
-            nc.sync.dma_start(out[n * P : (n + 1) * P, :], pages[n][:])
+        after3 = cut(after3[:, 0 : 2 * PACK * BLOCK])
+        for n in range(PACK):
+            place(2, n, after3[n])
+        place(3, 0, staging("y3", BLOCK)[:])
+        z.append(make_z2(4, after3[PACK:]))
+        for n, y_sb in enumerate(cut(staging("after4", 3 * BLOCK, "rows4"))):
+            place(3, 1 + n, y_sb)
+        z.append(make_z2(5, after3[PACK:]))
+        last = cut(staging("after5", 2 * BLOCK, "rows5"))
+        for step, (index, n) in enumerate(LAST_ORDER):
+            place(index, n, last[step % 2])
+            if index == 5:
+                nc.sync.dma_start(out[n * P : (n + 1) * P, :], pages[n][:])

@@ -14,16 +14,17 @@ FP4X4 = mybir.dt.float4_e2m1fn_x4
 ACT = mybir.ActivationFunctionType
 ALU = mybir.AluOpType
 
-K, K2, H, N, T, S, C, T2 = 1024, 512, 512, 512, 2048, 1024, 512, 2048
+K, K2, H, N = 1024, 512, 512, 512
+T, S, C = 2048, 1024, 512
 P = 128
 PACK = 4
+PASS = P * PACK
+LIST_ROWS = 16
+BANKS = 4
 FLOPS = 2 * (2 * K * H * S + K2 * H * C + H * N * (S + C))
 
-LAYER_BLOCKS = ((0, 256), (256, 512), (512, 1024))
-WB_SCALAR_SHARE = (4, 2)
-BLOCK = 256
-LAYER_Z = S // BLOCK
-LAST_ORDER = ((4, 0), (4, 1), (5, 0), (5, 1), (4, 2), (5, 2), (4, 3), (5, 3))
+BLOCK = S // 4
+STAGE_ONE = ((0, BLOCK), (BLOCK, 2 * BLOCK), (2 * BLOCK, S))
 
 
 def tile_list_treaty_layer_pages_kernel(
@@ -33,25 +34,32 @@ def tile_list_treaty_layer_pages_kernel(
     nc = tc.nc
     with ExitStack() as ctx:
         keep = ctx.enter_context(tc.tile_pool(name="keep", bufs=1))
-        y0_bytes = ctx.enter_context(tc.tile_pool(name="y0_bytes", bufs=1))
-        wo1_bytes = ctx.enter_context(tc.tile_pool(name="wo1_bytes", bufs=1))
-        psum = ctx.enter_context(tc.psum_pool(name="psum", bufs=2))
+        tab2_bytes = ctx.enter_context(tc.tile_pool(name="tab2_bytes", bufs=1))
+        psum = ctx.enter_context(tc.psum_pool(name="psum", bufs=BANKS))
 
-        def load_list(src, name):
-            tile = keep.tile(list(src.shape), U16, name=name)
+        def sbuf(name, width, dtype=F32, after=None):
+            return keep.tile([P, width], dtype, name=name, tag=after or name, align_bytes=64)
+
+        def cut(tile, width):
+            return [tile[:, c0 : c0 + width] for c0 in range(0, tile.shape[1], width)]
+
+        def entries(offsets, c0, c1):
+            return offsets[:, c0 // LIST_ROWS : c1 // LIST_ROWS]
+
+        def load(src, name, dtype=F32):
+            tile = keep.tile(list(src.shape), dtype, name=name)
             nc.sync.dma_start(tile[:], src)
             return tile
 
-        def zeroed_plane(width, name):
-            tile = keep.tile([P, width], U8, name=name, align_bytes=64)
-            nc.vector.memset(tile[:].bitcast(I32), 0)
-            return tile
+        def zeroed_plane(name, width, engine):
+            plane = sbuf(name, width, U8)
+            engine.memset(plane[:].bitcast(I32), 0)
+            return plane
 
-        def load_scale_rows(queue, plane, scales):
-            passes = scales.shape[0]
+        def load_scale_rows(plane, scales):
             for q in range(4):
-                queue.dma_start(
-                    plane[32 * q : 32 * q + 4, :].bitcast(I32).rearrange("r (a c) -> r a c", a=passes),
+                nc.sync.dma_start(
+                    plane[32 * q : 32 * q + 4, :].bitcast(I32).rearrange("r (a c) -> r a c", a=scales.shape[0]),
                     scales[:, 4 * q : 4 * q + 4, :].bitcast(I32).rearrange("a r c -> r a c"),
                 )
 
@@ -59,263 +67,227 @@ def tile_list_treaty_layer_pages_kernel(
             nc.sync.dma_start(tile[:], words.rearrange("p c i -> p (c i)").bitcast(I32))
             return tile
 
-        def staging(name, width, tag=None, dtype=F32):
-            return keep.tile([P, width], dtype, name=name, tag=tag or name, align_bytes=64)
+        def load_weight(rows, name, pieces):
+            width = rows.shape[1] // pieces
+            tiles = []
+            for piece in range(pieces):
+                raw = keep.tile([P, PACK, width], F32, name="%s%d" % (name, piece), align_bytes=64)
+                cols = rows[:, piece * width : (piece + 1) * width]
+                nc.sync.dma_start(raw[:], cols.rearrange("(p j) c -> p j c", j=PACK))
+                tiles.append(raw)
+            return tiles
 
-        def load_rows(rows, raw):
-            nc.sync.dma_start(raw[:], rows.rearrange("(p j) c -> p j c", j=PACK))
-            return raw
+        def gather(dst, window, offsets):
+            nc.vector.tensor_copy(dst[:], window.indirect(offsets))
+            return dst
 
-        def load_plain(src, name):
-            tile = keep.tile(list(src.shape), F32, name=name)
-            nc.sync.dma_start(tile[:], src)
-            return tile
+        def round_weight(copy, rounded, raws, piece, dealt):
+            order = "p (i m j) -> p m j i" if dealt else "p (m i j) -> p m j i"
+            step = P // len(raws)
+            copy(
+                rounded[:].rearrange(order, i=PACK, j=PACK)[:, piece * step : (piece + 1) * step],
+                raws[piece][:].rearrange("p j (m i) -> p m j i", i=PACK),
+            )
 
-        tab_plane = zeroed_plane(T, "tab_plane")
-        plane1 = keep.tile([P, S], U8, name="v_plane1", align_bytes=64)
-        nc.gpsimd.memset(plane1[:].bitcast(I32), 0)
-        w4_plane_in = zeroed_plane(2 * H, "w4_plane_in")
-        tab2_plane = zeroed_plane(T, "tab2_plane")
-        w8_plane = zeroed_plane(N, "w8_plane")
+        def quantize(values, codes, plane):
+            nc.vector.quantize_mx(out=codes.bitcast(FP8X4), scales=plane, in_=values[:])
+            return codes, plane
 
-        tab_sb = [load_words(tab_words[0], staging("tab_sb0", T, None, I32))]
-        offs_sb = load_list(offs, "offs_sb")
+        def matmul(acc, weight, slice_index, moving, start=True, stop=True):
+            cols = slice(slice_index * P, (slice_index + 1) * P)
+            nc.tensor.matmul_mx(
+                out=acc[:], lhsT=weight[0][:, cols].bitcast(FP8X4), lhsT_scale=weight[1][:, cols],
+                rhs=moving[0].bitcast(FP8X4), rhs_scale=moving[1], start=start, stop=stop,
+            )
+
+        tab_plane = zeroed_plane("tab_plane", T, nc.vector)
+        v_plane1 = zeroed_plane("v_plane1", S, nc.gpsimd)
+        w4_plane_in = zeroed_plane("w4_plane_in", 2 * H, nc.vector)
+        tab2_plane = zeroed_plane("tab2_plane", T, nc.vector)
+        w8_plane = zeroed_plane("w8_plane", N, nc.vector)
+
+        tab_sb = [load_words(tab_words[0], sbuf("tab_sb0", T, I32))]
+        offs_sb = load(offs, "offs_sb", U16)
         for q in range(4):
             nc.sync.dma_start(
                 tab_plane[32 * q : 32 * q + 8, :].bitcast(I32), tab_scales[:, 4 * q : 4 * q + 4, :].bitcast(I32)
             )
-        tab_sb.append(load_words(tab_words[1], staging("tab_sb1", T, None, I32)))
-        w4_in = keep.tile([P, 2 * 2 * H], U8, name="w4_in")
+        w4_in = sbuf("w4_in", 2 * 2 * H, U8)
         nc.sync.dma_start(
             w4_in[:].bitcast(I32).rearrange("p (a c) -> p a c", a=2),
             w4_words.bitcast(I32).rearrange("a p c -> p a c"),
         )
-        wb_raw = [load_rows(wb[0:512, :], keep.tile([P, PACK, H], F32, name="wb_raw0", align_bytes=64))]
-        load_scale_rows(nc.sync, w4_plane_in, w4_scales)
-        wb_raw.append(load_rows(wb[512:1024, :], keep.tile([P, PACK, H], F32, name="wb_raw1", align_bytes=64)))
+        wb_raw = [load_weight(wb[0:PASS, :], "wb_low", 1)]
+        tab_sb.append(load_words(tab_words[1], sbuf("tab_sb1", T, I32)))
+        load_scale_rows(w4_plane_in, w4_scales)
+        wb_raw.append(load_weight(wb[PASS:K, :], "wb_high", 2))
 
-        def gather(dst, window, offsets):
-            nc.vector.tensor_copy(dst, window.indirect(offsets))
+        v_words0 = gather(sbuf("v_words0", S, U32), tab_sb[0][:].bitcast(U32), offs_sb[:])
+        v_planes = gather(sbuf("v_planes", S, U8), tab_plane[:], offs_sb[:])
+        nc.sync.dma_start(v_plane1[0:100, :].bitcast(I32), v_planes[4:104, :].bitcast(I32))
 
-        def quantize(values, codes, name):
-            width = codes.shape[1]
-            plane = keep.tile([P, width], U8, name=name + "_plane", align_bytes=64)
-            nc.vector.quantize_mx(out=codes[:].bitcast(FP8X4), scales=plane[:], in_=values[:])
-            return codes, plane
+        gain_sb = load(gain.rearrange("(p t) -> p t", t=PACK), "gain_sb")
+        wo1_raw = load_weight(wo1, "wo1_raw", 2)
+        offs2_sb = load(offs2, "offs2_sb", U16)
+        load_scale_rows(tab2_plane, tab2_scales)
+        tab2_sb = load_words(tab2_words[0], tab2_bytes.tile([P, T], I32, name="tab2_sb", align_bytes=64, offset=0))
+        pages = [load(page1[0:P, :], "page0")]
+        offs3_sb = load(offs3, "offs3_sb", U16)
+        wg1_sb = [load(wg1[:, slice(*STAGE_ONE[0])], "wg1_sb0")]
+        pages.append(load(page1[P : 2 * P, :], "page1"))
+        pos1_sb = load(pos1, "pos1_sb", U16)
+        pages.append(load(page1[2 * P : 3 * P, :], "page2"))
+        wg1_sb.append(load(wg1[:, slice(*STAGE_ONE[1])], "wg1_sb1"))
+        wc_raw = load_weight(wc, "wc_raw", 2)
+        pages.append(load(page1[3 * P : 4 * P, :], "page3"))
+        wg1_sb.append(load(wg1[:, slice(*STAGE_ONE[2])], "wg1_sb2"))
+        offs4_sb = load(offs4, "offs4_sb", U16)
+        wg2_sb = load(wg2, "wg2_sb")
+        w8_sb = load_words(w8_words[0], sbuf("w8_sb", N, I32))
+        load_scale_rows(w8_plane, w8_scales)
 
-        def round_dealt(copy, grouped, raw, t0, t1):
-            copy(
-                grouped[:, t0 * H : t1 * H].rearrange("p (t m j) -> p m j t", t=t1 - t0, j=PACK),
-                raw[:].rearrange("p j (m t) -> p m j t", t=PACK)[:, :, :, t0:t1],
-            )
-
-        def quantize_weight(raw, name, tag, shares, codes_tag=None):
-            grouped = staging(name + "_grouped", PACK * H, tag, BF16)
-            for copy, t0, t1 in shares:
-                round_dealt(copy, grouped, raw, t0, t1)
-            return quantize(grouped, staging(name + "_codes", H, codes_tag, U32), name)
-
-        def gather_tab(source, dtype, c0, c1, name, tag=None):
-            tile = keep.tile([P, c1 - c0], dtype, name=name, tag=tag or name, align_bytes=64)
-            gather(tile[:], source, offs_sb[:, c0 // 16 : c1 // 16])
-            return tile
-
-        words0 = gather_tab(tab_sb[0][:].bitcast(U32), U32, 0, S, "v_words0")
-        plane0 = gather_tab(tab_plane[:], U8, 0, S, "v_plane0")
-        nc.sync.dma_start(plane1[0:100, :].bitcast(I32), plane0[4:104, :].bitcast(I32))
-
-        gain_sb = keep.tile([P, PACK], F32, name="gain_sb")
-        nc.sync.dma_start(gain_sb[:], gain.rearrange("(p t) -> p t", t=PACK))
-        wo1_raw = load_rows(wo1, keep.tile([P, PACK, N], F32, name="wo1_raw", align_bytes=64))
-        offs2_sb = load_list(offs2, "offs2_sb")
-        load_scale_rows(nc.sync, tab2_plane, tab2_scales)
-        pages = [load_plain(page1[0:P, :], "page0")]
-        offs3_sb = load_list(offs3, "offs3_sb")
-        wg1_sb = [load_plain(wg1[:, 0:256], "wg1_sb0")[:]]
-        pages.append(load_plain(page1[P : 2 * P, :], "page1"))
-        pos1_sb = load_list(pos1, "pos1_sb")
-        pages.append(load_plain(page1[2 * P : 3 * P, :], "page2"))
-        wg1_sb.append(load_plain(wg1[:, 256:512], "wg1_sb1")[:])
-        tab2_sb = load_words(tab2_words[0], staging("tab2_sb", T, None, I32))
-        pages.append(load_plain(page1[3 * P : 4 * P, :], "page3"))
-        wc_raw = load_rows(wc, keep.tile([P, PACK, H], F32, name="wc_raw", align_bytes=64))
-        wg1_high = load_plain(wg1[:, 512:1024], "wg1_sb2")
-        wg1_sb.extend([wg1_high[:, 0:BLOCK], wg1_high[:, BLOCK : 2 * BLOCK]])
-        offs4_sb = load_list(offs4, "offs4_sb")
-        wg2_all = load_plain(wg2, "wg2_sb")
-        wg2_sb = [wg2_all[:, 0:BLOCK], wg2_all[:, BLOCK : 2 * BLOCK]]
-        w8_sb = load_words(w8_words[0], staging("w8_sb", N, None, I32))
-        load_scale_rows(nc.sync, w8_plane, w8_scales)
-
-        w4_sb = keep.tile([P, 2 * 2 * H], U8, name="w4_sb", align_bytes=64)
+        w4_sb = sbuf("w4_sb", 2 * 2 * H, U8)
         nc.scalar.copy(
             w4_sb[:].bitcast(U16).rearrange("p (a t m) -> p a m t", a=2, t=PACK),
             w4_in[:].bitcast(U16).rearrange("p (a m t) -> p a m t", a=2, t=PACK),
         )
-        w4_plane = keep.tile([P, 2 * H], U8, name="w4_plane", align_bytes=64)
+        w4_plane = sbuf("w4_plane", 2 * H, U8)
         nc.vector.tensor_copy(
             w4_plane[:].rearrange("p (a t m) -> p a t m", a=2, t=PACK),
             w4_plane_in[:].rearrange("p (a m t) -> p a t m", a=2, t=PACK),
         )
-        words1 = {}
-        for index in (0, 2):
-            c0, c1 = LAYER_BLOCKS[index]
-            words1[index] = gather_tab(tab_sb[1][:].bitcast(U32), U32, c0, c1, "v_words1_%d" % index)[:]
-        on_scalar = [(nc.scalar.copy, 0, PACK)]
-        wb_q = [
-            quantize_weight(wb_raw[a], "wb%d" % a, "grouped%d" % a, [(nc.scalar.copy, 0, t), (nc.vector.tensor_copy, t, PACK)][: 1 if t == PACK else 2])
-            for a, t in enumerate(WB_SCALAR_SHARE)
-        ]
-        words1[1] = gather_tab(tab_sb[1][:].bitcast(U32), U32, *LAYER_BLOCKS[1], "v_words1_1", "grouped1")[:]
+        wb_mx = []
+        for a in range(2):
+            rounded = sbuf("wb_rounded%d" % a, PACK * H, BF16)
+            for piece in range(len(wb_raw[a])):
+                round_weight(nc.scalar.copy, rounded, wb_raw[a], piece, True)
+            wb_mx.append(quantize(rounded, sbuf("wb_codes%d" % a, H, U32)[:], sbuf("wb_plane%d" % a, H, U8)[:]))
+
+        v_words1 = {}
+        for block, after in ((0, None), (2, None), (1, "wb_rounded1")):
+            c0, c1 = STAGE_ONE[block]
+            dst = sbuf("v_words1_%d" % block, c1 - c0, U32, after)
+            v_words1[block] = gather(dst, tab_sb[1][:].bitcast(U32), entries(offs_sb, c0, c1))
 
         minus_two_gain = keep.tile([P, PACK], F32, name="minus_two_gain")
         nc.scalar.activation(minus_two_gain[:], gain_sb[:], ACT.Copy, scale=-2.0)
 
         h1 = [keep.tile([P, S], F32, name="h1_%d" % t) for t in range(PACK)]
 
-        def stage_one(index, left_sb):
-            c0, c1 = LAYER_BLOCKS[index]
-            width = c1 - c0
-            passes = (1, 0) if index == 1 else (0, 1)
-            v_codes = (words0[:, c0:c1].bitcast(FP8X4), words1[index].bitcast(FP8X4))
-            v_planes = (plane0[:, c0:c1], plane1[:, c0:c1])
-            v_planes_packed = (plane0[:, c0:c1], plane0[4:P, c0:c1])
-            for t in range(PACK):
-                left = psum.tile([P, width], F32, name="left", tag="scalar_bank", bufs=4)
-                right = psum.tile([P, width], F32, name="right", tag="vector_bank", bufs=4)
-                for a in passes:
+        def stage_one(block, left_tile):
+            c0, c1 = STAGE_ONE[block]
+            words = (v_words0[:, c0:c1], v_words1[block][:])
+            planes_from_0 = (v_planes[:, c0:c1], v_plane1[:, c0:c1])
+            planes_as_gathered = (v_planes[:, c0:c1], v_planes[4:P, c0:c1])
+            for t, left_sb in enumerate(cut(left_tile, c1 - c0)):
+                left = psum.tile([P, c1 - c0], F32, name="left", tag="scalar_bank")
+                right = psum.tile([P, c1 - c0], F32, name="right", tag="vector_bank")
+                for a in range(2):
                     col = a * H + t * P
                     nc.tensor.matmul_mx(
                         out=left[:],
-                        lhsT=w4_sb[:, 2 * col : 2 * (col + P)].bitcast(FP4X4),
-                        lhsT_scale=w4_plane[:, col : col + P],
-                        rhs=v_codes[a],
-                        rhs_scale=v_planes[a],
-                        start=(a == passes[0]), stop=(a == passes[1]),
+                        lhsT=w4_sb[:, 2 * col : 2 * (col + P)].bitcast(FP4X4), lhsT_scale=w4_plane[:, col : col + P],
+                        rhs=words[a].bitcast(FP8X4), rhs_scale=planes_from_0[a], start=(a == 0), stop=(a == 1),
                     )
-                for a in passes:
-                    codes, plane = wb_q[a]
-                    nc.tensor.matmul_mx(
-                        out=right[:],
-                        lhsT=codes[:, t * P : (t + 1) * P].bitcast(FP8X4),
-                        lhsT_scale=plane[:, t * P : (t + 1) * P],
-                        rhs=v_codes[a],
-                        rhs_scale=v_planes_packed[a],
-                        start=(a == passes[0]), stop=(a == passes[1]),
-                    )
-                nc.scalar.copy(left_sb[:, t * width : (t + 1) * width], left[:])
-                nc.vector.tensor_tensor(h1[t][:, c0:c1], right[:], left_sb[:, t * width : (t + 1) * width], ALU.mult)
+                for a in range(2):
+                    matmul(right, wb_mx[a], t, (words[a], planes_as_gathered[a]), start=(a == 0), stop=(a == 1))
+                nc.scalar.copy(left_sb, left[:])
+                nc.vector.tensor_tensor(h1[t][:, c0:c1], right[:], left_sb, ALU.mult)
 
-        def weave_and_quantize(rows, width, tag, name, codes):
-            woven = staging("woven", PACK * width, tag, BF16)
+        def weave_and_quantize(rows, name, codes, plane):
+            woven = sbuf(name, rows.shape[1], BF16)
             nc.scalar.copy(
                 woven[:].rearrange("p (c i t) -> p c t i", i=4, t=PACK),
                 rows[:].rearrange("p (t c i) -> p c t i", i=4, t=PACK),
             )
-            return quantize(woven, codes, name)
+            return quantize(woven, codes, plane)
 
-        def make_z1(index, tanh_slices, codes, rows=None):
-            c0 = index * BLOCK
-            if rows is None:
-                rows = staging("z_rows", PACK * BLOCK, "rows%d" % index, BF16)
-            for t in range(PACK):
-                nc.scalar.activation(tanh_slices[t], h1[t][:, c0 : c0 + BLOCK], ACT.Tanh)
-                nc.scalar.activation(
-                    rows[:, t * BLOCK : (t + 1) * BLOCK], tanh_slices[t], ACT.Copy, scale=gain_sb[:, t : t + 1]
-                )
-            return weave_and_quantize(rows, BLOCK, "woven%d" % index, "z%d" % index, codes)
+        def make_z1(block, tanh_tile, codes, plane):
+            rows = sbuf("rows%d" % block, PACK * BLOCK, BF16)
+            for t, (tanh, row) in enumerate(zip(cut(tanh_tile, BLOCK), cut(rows, BLOCK))):
+                nc.scalar.activation(tanh, h1[t][:, block * BLOCK : (block + 1) * BLOCK], ACT.Tanh)
+                nc.scalar.activation(row, tanh, ACT.Copy, scale=gain_sb[:, t : t + 1])
+            return weave_and_quantize(rows, "woven%d" % block, codes, plane)
 
-        def make_z2(index, half_slices):
-            c0 = (index - LAYER_Z) * BLOCK
-            rows = staging("z_rows", PACK * BLOCK, "rows%d" % index, BF16)
-            squares = cut(staging("squares", PACK * BLOCK, ("wb_raw1", "wo1_raw")[index - LAYER_Z]))
-            for t in range(PACK):
-                nc.scalar.activation(half_slices[t], shifted[t][:, c0 : c0 + BLOCK], ACT.Sin, scale=0.5)
-                nc.scalar.activation(squares[t], half_slices[t], ACT.Square)
-                nc.scalar.activation(
-                    rows[:, t * BLOCK : (t + 1) * BLOCK], squares[t], ACT.Identity,
-                    scale=minus_two_gain[:, t : t + 1], bias=gain_sb[:, t : t + 1],
-                )
-            return weave_and_quantize(rows, BLOCK, "woven%d" % index, "z%d" % index, staging("z%d_codes" % index, BLOCK, None, U32))
-
-        def place(index, n, y_sb):
-            if index < LAYER_Z:
-                (w_codes, w_plane), factors, offsets, c0 = wo1_q, wg1_sb[index], offs3_sb, index * BLOCK
-            else:
-                (w_codes, w_plane), factors, offsets, c0 = (w8_sb, w8_plane), wg2_sb[index - LAYER_Z], offs4_sb, (index - LAYER_Z) * BLOCK
-            z_codes, z_plane = z[index]
-            y = psum.tile([P, BLOCK], F32, name="y", tag="scalar_bank", bufs=4)
-            nc.tensor.matmul_mx(
-                out=y[:],
-                lhsT=w_codes[:, n * P : (n + 1) * P].bitcast(FP8X4),
-                lhsT_scale=w_plane[:, n * P : (n + 1) * P],
-                rhs=z_codes[:].bitcast(FP8X4),
-                rhs_scale=z_plane[:],
-                start=True, stop=True,
-            )
+        def place(n, weight, z, factors, offsets, y_sb):
+            y = psum.tile([P, y_sb.shape[1]], F32, name="y", tag="scalar_bank")
+            matmul(y, weight, n, z)
             nc.scalar.copy(y_sb, y[:])
-            window = pages[n][:].indirect(offsets[:, c0 // 16 : (c0 + BLOCK) // 16])
-            nc.vector.tensor_tensor(window, y_sb, factors, ALU.mult)
+            nc.vector.tensor_tensor(pages[n][:].indirect(offsets), y_sb, factors, ALU.mult)
 
-        def cut(tile, width=BLOCK):
-            return [tile[:, c0 : c0 + width] for c0 in range(0, tile.shape[1], width)]
+        def place_layers(n, block, part, y_sb):
+            c0 = STAGE_ONE[block][0]
+            z = (z1[block][0][:, part], z1[block][1][:, part])
+            place(n, wo1_mx, z, wg1_sb[block][:, part], entries(offs3_sb, c0 + part.start, c0 + part.stop), y_sb)
 
-        stage_one(0, staging("left0", PACK * BLOCK))
-        wo1_rounded = wo1_bytes.tile([P, PACK * N], BF16, name="wo1_rounded", align_bytes=64, offset=0)
-        nc.vector.tensor_copy(
-            wo1_rounded[:].rearrange("p (m i j) -> p m j i", i=4, j=PACK),
-            wo1_raw[:].rearrange("p j (m i) -> p m j i", i=4),
-        )
-        v2_plane = staging("v2_plane", C, None, U8)
-        gather(v2_plane[:], tab2_plane[:], offs2_sb[:])
-        wo1_q = quantize(wo1_rounded, staging("wo1_codes", N, "tab2_plane", U32), "wo1")
-        rows0 = wo1_bytes.tile([P, PACK * BLOCK], BF16, name="rows0", align_bytes=64, offset=16 * BLOCK)
-        z0_codes = wo1_bytes.tile([P, BLOCK], U32, name="z0_codes", align_bytes=64, offset=0)
-        z = [make_z1(0, cut(staging("tanh0", PACK * BLOCK)), z0_codes, rows0)]
+        low, high, both = slice(0, BLOCK), slice(BLOCK, 2 * BLOCK), slice(0, 2 * BLOCK)
 
-        stage_one(1, wo1_bytes.tile([P, PACK * BLOCK], F32, name="left1", align_bytes=64, offset=4 * BLOCK))
-        y0 = y0_bytes.tile([P, 3 * BLOCK], F32, name="y0", align_bytes=64, offset=0)
-        for n, y_sb in enumerate(cut(y0) + cut(staging("y0_last", BLOCK))):
-            place(0, n, y_sb)
-        z1_codes = y0_bytes.tile([P, BLOCK], U32, name="z1_codes", align_bytes=64, offset=0)
-        z.append(make_z1(1, cut(staging("tanh1", PACK * BLOCK, "tab_sb0")), z1_codes))
-        stage_one(2, y0_bytes.tile([P, PACK * 2 * BLOCK], F32, name="left2", align_bytes=64, offset=4 * BLOCK))
-        for n, y_sb in enumerate(cut(staging("y1", 2 * BLOCK))):
-            place(1, n, y_sb)
-        v2_words = staging("v2_words", C, None, U32)
-        gather(v2_words[:], tab2_sb[:].bitcast(U32), offs2_sb[:])
-        z.append(make_z1(2, cut(staging("tanh2", PACK * BLOCK, "rows1")), staging("z2_codes", BLOCK, None, U32)))
-        place(1, 2, staging("after2", BLOCK, "rows2")[:])
-        wc_codes, wc_plane = quantize_weight(wc_raw, "wc", "grouped0", on_scalar)
-        after_wc = cut(staging("after_wc", (1 + PACK) * BLOCK, "wc_raw"))
-        place(1, 3, after_wc[0])
-        z.append(make_z1(3, after_wc[1:], staging("z3_codes", BLOCK, None, U32)))
-        after3 = staging("after3", 2 * PACK * BLOCK + PACK * C, "rows3")
-        h2_sb = cut(after3[:, 2 * PACK * BLOCK :], C)
-        shifted = cut(staging("shifted", PACK * C, "woven1"), C)
-        for t in range(PACK):
-            h2 = psum.tile([P, C], F32, name="h2", tag="vector_bank", bufs=4)
-            nc.tensor.matmul_mx(
-                out=h2[:],
-                lhsT=wc_codes[:, t * P : (t + 1) * P].bitcast(FP8X4),
-                lhsT_scale=wc_plane[:, t * P : (t + 1) * P],
-                rhs=v2_words[:].bitcast(FP8X4),
-                rhs_scale=v2_plane[:],
-                start=True, stop=True,
+        wo1_rounded = sbuf("wo1_rounded", PACK * N, BF16, "wb_rounded0")
+        round_weight(nc.scalar.copy, wo1_rounded, wo1_raw, 0, False)
+        stage_one(0, sbuf("left0", PACK * BLOCK, F32, "wo1_raw0"))
+        round_weight(nc.vector.tensor_copy, wo1_rounded, wo1_raw, 1, False)
+        v2_plane = gather(sbuf("v2_plane", C, U8), tab2_plane[:], offs2_sb[:])
+        v2_words = gather(sbuf("v2_words", C, U32), tab2_sb[:].bitcast(U32), offs2_sb[:])
+        z0_codes = tab2_bytes.tile([P, BLOCK], U32, name="z0_codes", align_bytes=64, offset=0)
+        left1 = tab2_bytes.tile([P, PACK * BLOCK], F32, name="left1", align_bytes=64, offset=4 * BLOCK)
+        wo1_codes = tab2_bytes.tile([P, N], U32, name="wo1_codes", align_bytes=64, offset=4 * (1 + PACK) * BLOCK)
+        wo1_mx = quantize(wo1_rounded, wo1_codes[:], sbuf("wo1_plane", N, U8)[:])
+        z1 = [make_z1(0, sbuf("tanh0", PACK * BLOCK), z0_codes[:], sbuf("z0_plane", BLOCK, U8)[:])]
+
+        stage_one(1, left1)
+        for n, y_sb in enumerate(cut(sbuf("y0", 3 * BLOCK), BLOCK)):
+            place_layers(n, 0, low, y_sb)
+        z1_codes = sbuf("z1_codes", BLOCK, U32, "y0")
+        z1.append(make_z1(1, sbuf("tanh1", PACK * BLOCK, F32, "tab_sb0"), z1_codes[:], sbuf("z1_plane", BLOCK, U8)[:]))
+
+        wc_rounded = sbuf("wc_rounded", PACK * H, BF16, "wb_rounded0")
+        round_weight(nc.scalar.copy, wc_rounded, wc_raw, 0, True)
+        stage_one(2, sbuf("left2", PACK * 2 * BLOCK, F32, "wc_raw0"))
+        place_layers(0, 1, low, sbuf("y1", BLOCK)[:])
+        round_weight(nc.scalar.copy, wc_rounded, wc_raw, 1, True)
+        wc_mx = quantize(wc_rounded, sbuf("wc_codes", H, U32)[:], sbuf("wc_plane", H, U8)[:])
+        after_wc = cut(sbuf("after_wc", 2 * BLOCK, F32, "wc_raw1"), BLOCK)
+        place_layers(3, 0, low, after_wc[0])
+        place_layers(1, 1, low, after_wc[1])
+        after_weave1 = sbuf("after_weave1", PACK * BLOCK + PACK * C, F32, "rows1")
+        shifted = cut(sbuf("shifted", PACK * C, F32, "woven1"), C)
+        for t, h2_sb in enumerate(cut(after_weave1[:, PACK * BLOCK :], C)):
+            h2 = psum.tile([P, C], F32, name="h2", tag="vector_bank")
+            matmul(h2, wc_mx, t, (v2_words[:], v2_plane[:]))
+            nc.scalar.activation(h2_sb, h2[:], ACT.Copy, bias=-0.5 * math.pi)
+            nc.vector.tensor_tensor(shifted[t], h1[t][:].indirect(pos1_sb[:]), h2_sb, ALU.add)
+
+        z23_codes, z23_plane = sbuf("z23_codes", 2 * BLOCK, U32), sbuf("z23_plane", 2 * BLOCK, U8)
+        z1.append((z23_codes, z23_plane))
+        make_z1(2, after_weave1[:, 0 : PACK * BLOCK], z23_codes[:, low], z23_plane[:, low])
+        for n, y_sb in enumerate(cut(sbuf("after_weave2", 2 * BLOCK, F32, "rows2"), BLOCK)):
+            place_layers(2 + n, 1, low, y_sb)
+        make_z1(3, sbuf("tanh3", PACK * BLOCK, F32, "wb_low0"), z23_codes[:, high], z23_plane[:, high])
+        after_weave3 = sbuf("after_weave3", 2 * BLOCK + 2 * C, F32, "rows3")
+        for n, y_sb in enumerate(cut(after_weave3[:, both], BLOCK)):
+            place_layers(2 + n, 2, low, y_sb)
+
+        halves = cut(after_weave3[:, 2 * BLOCK :], C)
+        squares = cut(sbuf("squares", 2 * C, F32, "wb_high0"), C)
+        z2_rows = sbuf("z2_rows", PACK * C, BF16)
+
+        def make_z2_row(t):
+            nc.scalar.activation(halves[t % 2], shifted[t], ACT.Sin, scale=0.5)
+            nc.scalar.activation(squares[t % 2], halves[t % 2], ACT.Square)
+            nc.scalar.activation(
+                z2_rows[:, t * C : (t + 1) * C], squares[t % 2], ACT.Identity,
+                scale=minus_two_gain[:, t : t + 1], bias=gain_sb[:, t : t + 1],
             )
-            nc.scalar.activation(h2_sb[t], h2[:], ACT.Copy, bias=-0.5 * math.pi)
-            nc.vector.tensor_tensor(shifted[t], h1[t][:].indirect(pos1_sb[:]), h2_sb[t], ALU.add)
 
-        after3 = cut(after3[:, 0 : 2 * PACK * BLOCK])
-        for n in range(PACK):
-            place(2, n, after3[n])
-        place(3, 0, staging("y3", BLOCK)[:])
-        z.append(make_z2(4, after3[PACK:]))
-        for n, y_sb in enumerate(cut(staging("after4", 3 * BLOCK, "rows4"))):
-            place(3, 1 + n, y_sb)
-        z.append(make_z2(5, after3[PACK:]))
-        last = cut(staging("after5", 2 * BLOCK, "rows5"))
-        for step, (index, n) in enumerate(LAST_ORDER):
-            place(index, n, last[step % 2])
-            if index == 5:
-                nc.sync.dma_start(out[n * P : (n + 1) * P, :], pages[n][:])
+        make_z2_row(0)
+        for n, y_sb in enumerate(cut(sbuf("y23", 2 * 2 * BLOCK, F32, "tab_sb0"), 2 * BLOCK)):
+            place_layers(n, 2, both, y_sb)
+        place_layers(2, 2, high, sbuf("y3", BLOCK)[:])
+        for t in range(1, PACK):
+            make_z2_row(t)
+        z2 = weave_and_quantize(z2_rows, "z2_woven", sbuf("z2_codes", C, U32)[:], sbuf("z2_plane", C, U8)[:])
+        place_layers(3, 2, high, sbuf("after_z2_weave", BLOCK, F32, "z2_rows")[:])
+
+        for n, y_sb in enumerate(cut(sbuf("y2", PACK * C, F32, "tab_sb1"), C)):
+            place(n, (w8_sb, w8_plane), z2, wg2_sb[:], offs4_sb[:], y_sb)
+            nc.sync.dma_start(out[n * P : (n + 1) * P, :], pages[n][:])

import math
from contextlib import ExitStack

import concourse.mybir as mybir

F32 = mybir.dt.float32
BF16 = mybir.dt.bfloat16
I32 = mybir.dt.int32
U32 = mybir.dt.uint32
U16 = mybir.dt.uint16
U8 = mybir.dt.uint8
FP8X4 = mybir.dt.float8_e4m3fn_x4
FP4X4 = mybir.dt.float4_e2m1fn_x4
ACT = mybir.ActivationFunctionType
ALU = mybir.AluOpType

K, K2, H, N = 1024, 512, 512, 512
T, S, C = 2048, 1024, 512
P = 128
PACK = 4
PASS = P * PACK
LIST_ROWS = 16
BANKS = 4
FLOPS = 2 * (2 * K * H * S + K2 * H * C + H * N * (S + C))

BLOCK = S // 4
STAGE_ONE = ((0, BLOCK), (BLOCK, 2 * BLOCK), (2 * BLOCK, S))


def tile_list_treaty_layer_pages_kernel(
    tc, tab_words, tab_scales, tab2_words, tab2_scales, offs, offs2, pos1, offs3, offs4,
    w4_words, w4_scales, wb, wc, gain, wo1, w8_words, w8_scales, wg1, wg2, page1, out,
):
    nc = tc.nc
    with ExitStack() as ctx:
        keep = ctx.enter_context(tc.tile_pool(name="keep", bufs=1))
        tab2_bytes = ctx.enter_context(tc.tile_pool(name="tab2_bytes", bufs=1))
        psum = ctx.enter_context(tc.psum_pool(name="psum", bufs=BANKS))

        def sbuf(name, width, dtype=F32, after=None):
            return keep.tile([P, width], dtype, name=name, tag=after or name, align_bytes=64)

        def cut(tile, width):
            return [tile[:, c0 : c0 + width] for c0 in range(0, tile.shape[1], width)]

        def entries(offsets, c0, c1):
            return offsets[:, c0 // LIST_ROWS : c1 // LIST_ROWS]

        def load(src, name, dtype=F32):
            tile = keep.tile(list(src.shape), dtype, name=name)
            nc.sync.dma_start(tile[:], src)
            return tile

        def zeroed_plane(name, width, engine):
            plane = sbuf(name, width, U8)
            engine.memset(plane[:].bitcast(I32), 0)
            return plane

        def load_scale_rows(plane, scales):
            for q in range(4):
                nc.sync.dma_start(
                    plane[32 * q : 32 * q + 4, :].bitcast(I32).rearrange("r (a c) -> r a c", a=scales.shape[0]),
                    scales[:, 4 * q : 4 * q + 4, :].bitcast(I32).rearrange("a r c -> r a c"),
                )

        def load_words(words, tile):
            nc.sync.dma_start(tile[:], words.rearrange("p c i -> p (c i)").bitcast(I32))
            return tile

        def load_weight(rows, name, pieces):
            width = rows.shape[1] // pieces
            tiles = []
            for piece in range(pieces):
                raw = keep.tile([P, PACK, width], F32, name="%s%d" % (name, piece), align_bytes=64)
                cols = rows[:, piece * width : (piece + 1) * width]
                nc.sync.dma_start(raw[:], cols.rearrange("(p j) c -> p j c", j=PACK))
                tiles.append(raw)
            return tiles

        def gather(dst, window, offsets):
            nc.vector.tensor_copy(dst[:], window.indirect(offsets))
            return dst

        def round_weight(copy, rounded, raws, piece, dealt):
            order = "p (i m j) -> p m j i" if dealt else "p (m i j) -> p m j i"
            step = P // len(raws)
            copy(
                rounded[:].rearrange(order, i=PACK, j=PACK)[:, piece * step : (piece + 1) * step],
                raws[piece][:].rearrange("p j (m i) -> p m j i", i=PACK),
            )

        def quantize(values, codes, plane):
            nc.vector.quantize_mx(out=codes.bitcast(FP8X4), scales=plane, in_=values[:])
            return codes, plane

        def matmul(acc, weight, slice_index, moving, start=True, stop=True):
            cols = slice(slice_index * P, (slice_index + 1) * P)
            nc.tensor.matmul_mx(
                out=acc[:], lhsT=weight[0][:, cols].bitcast(FP8X4), lhsT_scale=weight[1][:, cols],
                rhs=moving[0].bitcast(FP8X4), rhs_scale=moving[1], start=start, stop=stop,
            )

        tab_plane = zeroed_plane("tab_plane", T, nc.vector)
        v_plane1 = zeroed_plane("v_plane1", S, nc.gpsimd)
        w4_plane_in = zeroed_plane("w4_plane_in", 2 * H, nc.vector)
        tab2_plane = zeroed_plane("tab2_plane", T, nc.vector)
        w8_plane = zeroed_plane("w8_plane", N, nc.vector)

        tab_sb = [load_words(tab_words[0], sbuf("tab_sb0", T, I32))]
        offs_sb = load(offs, "offs_sb", U16)
        for q in range(4):
            nc.sync.dma_start(
                tab_plane[32 * q : 32 * q + 8, :].bitcast(I32), tab_scales[:, 4 * q : 4 * q + 4, :].bitcast(I32)
            )
        w4_in = sbuf("w4_in", 2 * 2 * H, U8)
        nc.sync.dma_start(
            w4_in[:].bitcast(I32).rearrange("p (a c) -> p a c", a=2),
            w4_words.bitcast(I32).rearrange("a p c -> p a c"),
        )
        wb_raw = [load_weight(wb[0:PASS, :], "wb_low", 1)]
        tab_sb.append(load_words(tab_words[1], sbuf("tab_sb1", T, I32)))
        load_scale_rows(w4_plane_in, w4_scales)
        wb_raw.append(load_weight(wb[PASS:K, :], "wb_high", 2))

        v_words0 = gather(sbuf("v_words0", S, U32), tab_sb[0][:].bitcast(U32), offs_sb[:])
        v_planes = gather(sbuf("v_planes", S, U8), tab_plane[:], offs_sb[:])
        nc.sync.dma_start(v_plane1[0:100, :].bitcast(I32), v_planes[4:104, :].bitcast(I32))

        gain_sb = load(gain.rearrange("(p t) -> p t", t=PACK), "gain_sb")
        wo1_raw = load_weight(wo1, "wo1_raw", 2)
        offs2_sb = load(offs2, "offs2_sb", U16)
        load_scale_rows(tab2_plane, tab2_scales)
        tab2_sb = load_words(tab2_words[0], tab2_bytes.tile([P, T], I32, name="tab2_sb", align_bytes=64, offset=0))
        pages = [load(page1[0:P, :], "page0")]
        offs3_sb = load(offs3, "offs3_sb", U16)
        wg1_sb = [load(wg1[:, slice(*STAGE_ONE[0])], "wg1_sb0")]
        pages.append(load(page1[P : 2 * P, :], "page1"))
        pos1_sb = load(pos1, "pos1_sb", U16)
        pages.append(load(page1[2 * P : 3 * P, :], "page2"))
        wg1_sb.append(load(wg1[:, slice(*STAGE_ONE[1])], "wg1_sb1"))
        wc_raw = load_weight(wc, "wc_raw", 2)
        pages.append(load(page1[3 * P : 4 * P, :], "page3"))
        wg1_sb.append(load(wg1[:, slice(*STAGE_ONE[2])], "wg1_sb2"))
        offs4_sb = load(offs4, "offs4_sb", U16)
        wg2_sb = load(wg2, "wg2_sb")
        w8_sb = load_words(w8_words[0], sbuf("w8_sb", N, I32))
        load_scale_rows(w8_plane, w8_scales)

        w4_sb = sbuf("w4_sb", 2 * 2 * H, U8)
        nc.scalar.copy(
            w4_sb[:].bitcast(U16).rearrange("p (a t m) -> p a m t", a=2, t=PACK),
            w4_in[:].bitcast(U16).rearrange("p (a m t) -> p a m t", a=2, t=PACK),
        )
        w4_plane = sbuf("w4_plane", 2 * H, U8)
        nc.vector.tensor_copy(
            w4_plane[:].rearrange("p (a t m) -> p a t m", a=2, t=PACK),
            w4_plane_in[:].rearrange("p (a m t) -> p a t m", a=2, t=PACK),
        )
        wb_mx = []
        for a in range(2):
            rounded = sbuf("wb_rounded%d" % a, PACK * H, BF16)
            for piece in range(len(wb_raw[a])):
                round_weight(nc.scalar.copy, rounded, wb_raw[a], piece, True)
            wb_mx.append(quantize(rounded, sbuf("wb_codes%d" % a, H, U32)[:], sbuf("wb_plane%d" % a, H, U8)[:]))

        v_words1 = {}
        for block, after in ((0, None), (2, None), (1, "wb_rounded1")):
            c0, c1 = STAGE_ONE[block]
            dst = sbuf("v_words1_%d" % block, c1 - c0, U32, after)
            v_words1[block] = gather(dst, tab_sb[1][:].bitcast(U32), entries(offs_sb, c0, c1))

        minus_two_gain = keep.tile([P, PACK], F32, name="minus_two_gain")
        nc.scalar.activation(minus_two_gain[:], gain_sb[:], ACT.Copy, scale=-2.0)

        h1 = [keep.tile([P, S], F32, name="h1_%d" % t) for t in range(PACK)]

        def stage_one(block, left_tile):
            c0, c1 = STAGE_ONE[block]
            words = (v_words0[:, c0:c1], v_words1[block][:])
            planes_from_0 = (v_planes[:, c0:c1], v_plane1[:, c0:c1])
            planes_as_gathered = (v_planes[:, c0:c1], v_planes[4:P, c0:c1])
            for t, left_sb in enumerate(cut(left_tile, c1 - c0)):
                left = psum.tile([P, c1 - c0], F32, name="left", tag="scalar_bank")
                right = psum.tile([P, c1 - c0], F32, name="right", tag="vector_bank")
                for a in range(2):
                    col = a * H + t * P
                    nc.tensor.matmul_mx(
                        out=left[:],
                        lhsT=w4_sb[:, 2 * col : 2 * (col + P)].bitcast(FP4X4), lhsT_scale=w4_plane[:, col : col + P],
                        rhs=words[a].bitcast(FP8X4), rhs_scale=planes_from_0[a], start=(a == 0), stop=(a == 1),
                    )
                for a in range(2):
                    matmul(right, wb_mx[a], t, (words[a], planes_as_gathered[a]), start=(a == 0), stop=(a == 1))
                nc.scalar.copy(left_sb, left[:])
                nc.vector.tensor_tensor(h1[t][:, c0:c1], right[:], left_sb, ALU.mult)

        def weave_and_quantize(rows, name, codes, plane):
            woven = sbuf(name, rows.shape[1], BF16)
            nc.scalar.copy(
                woven[:].rearrange("p (c i t) -> p c t i", i=4, t=PACK),
                rows[:].rearrange("p (t c i) -> p c t i", i=4, t=PACK),
            )
            return quantize(woven, codes, plane)

        def make_z1(block, tanh_tile, codes, plane):
            rows = sbuf("rows%d" % block, PACK * BLOCK, BF16)
            for t, (tanh, row) in enumerate(zip(cut(tanh_tile, BLOCK), cut(rows, BLOCK))):
                nc.scalar.activation(tanh, h1[t][:, block * BLOCK : (block + 1) * BLOCK], ACT.Tanh)
                nc.scalar.activation(row, tanh, ACT.Copy, scale=gain_sb[:, t : t + 1])
            return weave_and_quantize(rows, "woven%d" % block, codes, plane)

        def place(n, weight, z, factors, offsets, y_sb):
            y = psum.tile([P, y_sb.shape[1]], F32, name="y", tag="scalar_bank")
            matmul(y, weight, n, z)
            nc.scalar.copy(y_sb, y[:])
            nc.vector.tensor_tensor(pages[n][:].indirect(offsets), y_sb, factors, ALU.mult)

        def place_layers(n, block, part, y_sb):
            c0 = STAGE_ONE[block][0]
            z = (z1[block][0][:, part], z1[block][1][:, part])
            place(n, wo1_mx, z, wg1_sb[block][:, part], entries(offs3_sb, c0 + part.start, c0 + part.stop), y_sb)

        low, high, both = slice(0, BLOCK), slice(BLOCK, 2 * BLOCK), slice(0, 2 * BLOCK)

        wo1_rounded = sbuf("wo1_rounded", PACK * N, BF16, "wb_rounded0")
        round_weight(nc.scalar.copy, wo1_rounded, wo1_raw, 0, False)
        stage_one(0, sbuf("left0", PACK * BLOCK, F32, "wo1_raw0"))
        round_weight(nc.vector.tensor_copy, wo1_rounded, wo1_raw, 1, False)
        v2_plane = gather(sbuf("v2_plane", C, U8), tab2_plane[:], offs2_sb[:])
        v2_words = gather(sbuf("v2_words", C, U32), tab2_sb[:].bitcast(U32), offs2_sb[:])
        z0_codes = tab2_bytes.tile([P, BLOCK], U32, name="z0_codes", align_bytes=64, offset=0)
        left1 = tab2_bytes.tile([P, PACK * BLOCK], F32, name="left1", align_bytes=64, offset=4 * BLOCK)
        wo1_codes = tab2_bytes.tile([P, N], U32, name="wo1_codes", align_bytes=64, offset=4 * (1 + PACK) * BLOCK)
        wo1_mx = quantize(wo1_rounded, wo1_codes[:], sbuf("wo1_plane", N, U8)[:])
        z1 = [make_z1(0, sbuf("tanh0", PACK * BLOCK), z0_codes[:], sbuf("z0_plane", BLOCK, U8)[:])]

        stage_one(1, left1)
        for n, y_sb in enumerate(cut(sbuf("y0", 3 * BLOCK), BLOCK)):
            place_layers(n, 0, low, y_sb)
        z1_codes = sbuf("z1_codes", BLOCK, U32, "y0")
        z1.append(make_z1(1, sbuf("tanh1", PACK * BLOCK, F32, "tab_sb0"), z1_codes[:], sbuf("z1_plane", BLOCK, U8)[:]))

        wc_rounded = sbuf("wc_rounded", PACK * H, BF16, "wb_rounded0")
        round_weight(nc.scalar.copy, wc_rounded, wc_raw, 0, True)
        stage_one(2, sbuf("left2", PACK * 2 * BLOCK, F32, "wc_raw0"))
        place_layers(0, 1, low, sbuf("y1", BLOCK)[:])
        round_weight(nc.scalar.copy, wc_rounded, wc_raw, 1, True)
        wc_mx = quantize(wc_rounded, sbuf("wc_codes", H, U32)[:], sbuf("wc_plane", H, U8)[:])
        after_wc = cut(sbuf("after_wc", 2 * BLOCK, F32, "wc_raw1"), BLOCK)
        place_layers(3, 0, low, after_wc[0])
        place_layers(1, 1, low, after_wc[1])
        after_weave1 = sbuf("after_weave1", PACK * BLOCK + PACK * C, F32, "rows1")
        shifted = cut(sbuf("shifted", PACK * C, F32, "woven1"), C)
        for t, h2_sb in enumerate(cut(after_weave1[:, PACK * BLOCK :], C)):
            h2 = psum.tile([P, C], F32, name="h2", tag="vector_bank")
            matmul(h2, wc_mx, t, (v2_words[:], v2_plane[:]))
            nc.scalar.activation(h2_sb, h2[:], ACT.Copy, bias=-0.5 * math.pi)
            nc.vector.tensor_tensor(shifted[t], h1[t][:].indirect(pos1_sb[:]), h2_sb, ALU.add)

        z23_codes, z23_plane = sbuf("z23_codes", 2 * BLOCK, U32), sbuf("z23_plane", 2 * BLOCK, U8)
        z1.append((z23_codes, z23_plane))
        make_z1(2, after_weave1[:, 0 : PACK * BLOCK], z23_codes[:, low], z23_plane[:, low])
        for n, y_sb in enumerate(cut(sbuf("after_weave2", 2 * BLOCK, F32, "rows2"), BLOCK)):
            place_layers(2 + n, 1, low, y_sb)
        make_z1(3, sbuf("tanh3", PACK * BLOCK, F32, "wb_low0"), z23_codes[:, high], z23_plane[:, high])
        after_weave3 = sbuf("after_weave3", 2 * BLOCK + 2 * C, F32, "rows3")
        for n, y_sb in enumerate(cut(after_weave3[:, both], BLOCK)):
            place_layers(2 + n, 2, low, y_sb)

        halves = cut(after_weave3[:, 2 * BLOCK :], C)
        squares = cut(sbuf("squares", 2 * C, F32, "wb_high0"), C)
        z2_rows = sbuf("z2_rows", PACK * C, BF16)

        def make_z2_row(t):
            nc.scalar.activation(halves[t % 2], shifted[t], ACT.Sin, scale=0.5)
            nc.scalar.activation(squares[t % 2], halves[t % 2], ACT.Square)
            nc.scalar.activation(
                z2_rows[:, t * C : (t + 1) * C], squares[t % 2], ACT.Identity,
                scale=minus_two_gain[:, t : t + 1], bias=gain_sb[:, t : t + 1],
            )

        make_z2_row(0)
        for n, y_sb in enumerate(cut(sbuf("y23", 2 * 2 * BLOCK, F32, "tab_sb0"), 2 * BLOCK)):
            place_layers(n, 2, both, y_sb)
        place_layers(2, 2, high, sbuf("y3", BLOCK)[:])
        for t in range(1, PACK):
            make_z2_row(t)
        z2 = weave_and_quantize(z2_rows, "z2_woven", sbuf("z2_codes", C, U32)[:], sbuf("z2_plane", C, U8)[:])
        place_layers(3, 2, high, sbuf("after_z2_weave", BLOCK, F32, "z2_rows")[:])

        for n, y_sb in enumerate(cut(sbuf("y2", PACK * C, F32, "tab_sb1"), C)):
            place(n, (w8_sb, w8_plane), z2, wg2_sb[:], offs4_sb[:], y_sb)
            nc.sync.dma_start(out[n * P : (n + 1) * P, :], pages[n][:])
